import numpy as np
import ml_dtypes


def mxq(x, axis, fmt="e4m3"):
    dtype, down = {"e4m3": (ml_dtypes.float8_e4m3fn, 7), "e5m2": (ml_dtypes.float8_e5m2, 14)}[fmt]
    v = np.moveaxis(np.asarray(x, np.float32).astype(ml_dtypes.bfloat16).astype(np.float64), axis, -1)
    blocks = v.reshape(v.shape[:-1] + (-1, 32))
    amax = np.abs(blocks).max(-1, keepdims=True)
    byte = np.maximum(np.where(amax > 0, np.frexp(amax)[1] - 1 + 127, 0) - down, 1)
    scale = np.exp2(byte - 127.0)
    codes = (blocks / scale).astype(np.float32).astype(dtype).astype(np.float64)
    return np.moveaxis((codes * scale).reshape(v.shape), -1, axis)


WIDE = False


def mx_kscale(k):
    if not WIDE:
        return np.ones(k)
    levels = np.array([10, -10, 5, -5, 0])
    if k % 512:
        return np.exp2(np.random.permutation(np.resize(levels, k // 32))).repeat(32)
    a = np.empty((k // 512, 16))
    for p in range(k // 512):
        a[p, :8] = np.random.permutation(np.resize(levels, 8))
        for g in range(8):
            far = levels[np.abs(levels - a[p, g]) >= 10]
            a[p, g + 8] = far[np.random.randint(len(far))]
    return np.exp2(a.ravel()).repeat(32)


def f64(x):
    return np.asarray(x).astype(np.float64)


def striped(idx):
    return np.tile(idx.reshape(-1, 16).T, (8, 1)).astype(np.uint16)


def unstriped(offs):
    return offs[:16].T.reshape(-1).astype(np.int64)


def sigmoid(v):
    return 1.0 / (1.0 + np.exp(-np.maximum(v, -700.0)))

def planes(y):
    n, m = y.shape
    v = y.astype(np.float32).astype(ml_dtypes.bfloat16).astype(np.float64).reshape(n // 32, 32, m)
    top = np.abs(v).max(1)
    byte = np.clip(np.where(top > 0, np.frexp(top)[1] - 1 + 127 - 7, 1), 1, 254)
    codes = (v * np.exp2(127.0 - byte)[:, None, :]).reshape(n, m).astype(np.float32).astype(ml_dtypes.float8_e4m3fn).view(np.uint8)
    words = codes.reshape(n // 512, 128, 4, m).transpose(0, 1, 3, 2)
    return np.ascontiguousarray(words), np.ascontiguousarray(byte.astype(np.uint8).reshape(n // 512, 16, m))


K, T, S, N, U = 512, 1024, 512, 512, 1024


def setup_inputs():
    n = np.random.standard_normal
    s = mx_kscale(K)[:, None]
    return {
        "xT": (n((K, T)) * s).astype(np.float32),
        "mem": n((N, U)).astype(np.float32),
        "w1": (n((K, N)) / np.sqrt(K) / s).astype(np.float32),
        "w2": (n((K, N)) / np.sqrt(K) / s).astype(np.float32),
        "offs": striped(np.random.permutation(T)[:S]),
        "slot": striped(np.random.permutation(U)[:S]),
    }


def reference(xT, mem, w1, w2, offs, slot):
    old = f64(mem)[:, unstriped(slot)]
    xq = mxq(f64(xT)[:, unstriped(offs)], 0, "e4m3")
    g = sigmoid(mxq(f64(w2), 0, "e4m3").T @ xq)
    y = np.tanh(mxq(f64(w1), 0, "e4m3").T @ xq)
    out = f64(mem).copy()
    out[:, unstriped(slot)] = old + g * (y - old)
    return (out,) + planes(out)

@@ -1,0 +1,178 @@
+from contextlib import ExitStack
+
+import concourse.mybir as mybir
+
+K, T, S, N, U = 512, 1024, 512, 512, 1024
+FLOPS = 2 * 2 * K * N * S
+
+F32 = mybir.dt.float32
+BF16 = mybir.dt.bfloat16
+I32 = mybir.dt.int32
+U32 = mybir.dt.uint32
+U16 = mybir.dt.uint16
+U8 = mybir.dt.uint8
+FP8X4 = mybir.dt.float8_e4m3fn_x4
+ALU = mybir.AluOpType
+ACT = mybir.ActivationFunctionType
+
+P = 128
+PACK = 4
+CHUNK = 256
+X_SPLIT = 340
+
+
+def tile_picked_gmem_tanh_lo_kernel(tc, xT, mem, w1, w2, offs, slot, out_0, out_1, out_2):
+    nc = tc.nc
+    with ExitStack() as ctx:
+        keep = ctx.enter_context(tc.tile_pool(name="keep", bufs=1))
+        psum = ctx.enter_context(tc.psum_pool(name="psum", bufs=1))
+
+        offs_t = keep.tile([P, S // 16], U16, name="offs_t")
+        slot_t = keep.tile([P, S // 16], U16, name="slot_t")
+        x_raw = [keep.tile([P, T], F32, name=f"x_raw{j}") for j in range(PACK)]
+        w1_raw = keep.tile([P, PACK, N], F32, name="w1_raw")
+        w2_raw = keep.tile([P, PACK, N], F32, name="w2_raw")
+        page = [keep.tile([P, U], F32, name=f"page{t}") for t in range(PACK)]
+
+        x_rows = xT.rearrange("(p j) c -> p j c", j=PACK)
+        mem_rows = mem.rearrange("(p t) c -> p t c", t=PACK)
+        out_rows = out_0.rearrange("(p t) c -> p t c", t=PACK)
+
+        nc.sync.dma_start(offs_t[:], offs)
+        for j in range(PACK):
+            nc.sync.dma_start(x_raw[j][:], x_rows[:, j, :])
+        nc.sync.dma_start(w1_raw[:], w1.rearrange("(p j) c -> p j c", j=PACK))
+        nc.sync.dma_start(w2_raw[:], w2.rearrange("(p j) c -> p j c", j=PACK))
+        nc.sync.dma_start(slot_t[:], slot)
+        for t in range(PACK):
+            nc.sync.dma_start(page[t][:], mem_rows[:, t, :])
+
+        warm_in = keep.tile([P, 1], F32, name="warm_in")
+        warm_out = keep.tile([P, 1], F32, name="warm_out")
+        nc.gpsimd.memset(warm_in[:], 0.0)
+        nc.scalar.activation(warm_out[:], warm_in[:], ACT.Sigmoid)
+
+        picked = [keep.tile([P, 2, S], F32, name=f"picked{h}") for h in range(2)]
+        x_bf = keep.tile([P, S, PACK], BF16, name="x_bf", align_bytes=64)
+
+        def weave_x(copy, h, lo, hi):
+            copy(x_bf[:, lo:hi, 2 * h : 2 * h + 2], picked[h][:, :, lo:hi].rearrange("p e c -> p c e"))
+
+        for j in range(PACK):
+            nc.vector.tensor_copy(picked[j // 2][:, j % 2, :], x_raw[j][:].indirect(offs_t[:]))
+            if j == 1:
+                weave_x(nc.scalar.copy, 0, 0, S)
+        weave_x(nc.vector.tensor_copy, 1, 0, X_SPLIT)
+        weave_x(nc.scalar.copy, 1, X_SPLIT, S)
+
+        x_codes = keep.tile([P, S], U32, name="x_codes", align_bytes=64)
+        x_scales = keep.tile([P, S], U8, name="x_scales", align_bytes=64)
+        nc.vector.quantize_mx(x_codes[:].bitcast(FP8X4), x_scales[:], x_bf[:].rearrange("p c j -> p (c j)"))
+
+        def deal(copy, raw, t0, t1, name, tag):
+            dealt = keep.tile([P, t1 - t0, P, PACK], BF16, name=name, tag=tag, align_bytes=64)
+            copy(dealt[:].rearrange("p t m j -> p m t j"), raw[:].rearrange("p j (m t) -> p m t j", t=PACK)[:, :, t0:t1, :])
+            return dealt
+
+        stationary = {}
+
+        def quantize_w(which, dealt, first, t0, t1, tag):
+            width = (t1 - t0) * P
+            codes = keep.tile([P, width], U32, name=f"{which}_codes{t0}", tag=tag, align_bytes=64)
+            scales = keep.tile([P, width], U8, name=f"{which}_scales{t0}", align_bytes=64)
+            nc.vector.quantize_mx(
+                codes[:].bitcast(FP8X4), scales[:], dealt[:, t0 - first : t1 - first, :, :].rearrange("p t m j -> p (t m j)")
+            )
+            for t in range(t0, t1):
+                cols = slice((t - t0) * P, (t - t0 + 1) * P)
+                stationary[which, t] = (codes[:, cols], scales[:, cols])
+
+        def product(which, t, bank):
+            acc = psum.tile([P, S], F32, name=f"{which}_acc{t}", tag=bank)
+            codes, scales = stationary[which, t]
+            nc.tensor.matmul_mx(
+                acc[:],
+                lhsT=codes.bitcast(FP8X4),
+                lhsT_scale=scales,
+                rhs=x_codes[:].bitcast(FP8X4),
+                rhs_scale=x_scales[:],
+                start=True,
+                stop=True,
+            )
+            return acc
+
+        cand = [keep.tile([P, S], F32, name=f"cand{t}") for t in range(PACK)]
+        stay = [keep.tile([P, S], F32, name=f"stay{t}") for t in range(PACK)]
+        diff = [keep.tile([P, S], F32, name=f"diff{t}", tag="late" if t == 0 else f"diff{t}", align_bytes=64) for t in range(PACK)]
+        kept = [keep.tile([P, S], F32, name=f"kept{t}") for t in range(PACK)]
+        chunks = U // CHUNK
+        y_bf = [keep.tile([P, CHUNK, PACK], BF16, name=f"y_bf{c}", align_bytes=64) for c in range(chunks)]
+
+        def candidate(t, bank):
+            nc.scalar.activation(cand[t][:], product("w1", t, bank)[:], ACT.Tanh)
+
+        def gate(t, bank):
+            nc.scalar.activation(stay[t][:], product("w2", t, bank)[:], ACT.Sigmoid, scale=-1.0)
+
+        def look_up(t):
+            nc.vector.tensor_tensor(diff[t][:], page[t][:].indirect(slot_t[:]), cand[t][:], ALU.subtract)
+
+        def weigh(t):
+            nc.vector.tensor_tensor(kept[t][:], diff[t][:], stay[t][:], ALU.mult)
+
+        def put(t):
+            nc.vector.tensor_tensor(page[t][:].indirect(slot_t[:]), kept[t][:], cand[t][:], ALU.add)
+            nc.sync.dma_start(out_rows[:, t, :], page[t][:])
+
+        def round_out(copy, t, c):
+            src = page[t][:, c * CHUNK : (c + 1) * CHUNK]
+            if t == 2 and c % 2 == 0:
+                copy(y_bf[c][:, :, 2:4], src.unsqueeze(2).to_broadcast([P, CHUNK, 2]))
+            else:
+                copy(y_bf[c][:, :, t], src)
+
+        w1_first = deal(nc.vector.tensor_copy, w1_raw, 0, 1, "w1_first", "w1_first")
+        w1_rest = deal(nc.scalar.copy, w1_raw, 1, PACK, "w1_rest", "w1_rest")
+        quantize_w("w1", w1_first, 0, 0, 1, "w1_codes0")
+        candidate(0, "a")
+        quantize_w("w1", w1_rest, 1, 1, 2, "w1_codes1")
+        quantize_w("w1", w1_rest, 1, 2, 4, "w1_codes2")
+        w2_first = deal(nc.vector.tensor_copy, w2_raw, 0, 1, "w2_first", "w2_first")
+        w2_mid = deal(nc.scalar.copy, w2_raw, 1, 3, "w2_mid", "w2_mid")
+        quantize_w("w2", w2_first, 0, 0, 1, "w2_codes0")
+        gate(0, "b")
+        look_up(0)
+        candidate(1, "c")
+        candidate(2, "b")
+        candidate(3, "b")
+        for t in range(PACK):
+            weigh(t)
+            if t + 1 < PACK:
+                look_up(t + 1)
+            if t == 0:
+                quantize_w("w2", w2_mid, 1, 1, 3, "late")
+                gate(1, "a")
+                gate(2, "a")
+                w2_last = deal(nc.scalar.copy, w2_raw, 3, 4, "w2_last", "late")
+            if t == 1:
+                quantize_w("w2", w2_last, 3, 3, 4, "w2_codes3")
+                gate(3, "a")
+            put(t)
+            if t + 1 < PACK:
+                for c in range(chunks):
+                    round_out(nc.scalar.copy, t, c)
+
+        y_codes = keep.tile([P, U], U32, name="y_codes", align_bytes=64)
+        y_scales = keep.tile([P, U], U8, name="y_scales", align_bytes=64)
+        words = out_1.rearrange("z l c r -> (z l) (c r)").bitcast(I32)
+        last = PACK - 1
+        for c in range(chunks):
+            round_out(nc.scalar.copy if c % 2 else nc.vector.tensor_copy, last, c)
+        for c in range(chunks):
+            cols = slice(c * CHUNK, (c + 1) * CHUNK)
+            nc.vector.quantize_mx(y_codes[:, cols].bitcast(FP8X4), y_scales[:, cols], y_bf[c][:].rearrange("p c r -> p (c r)"))
+            nc.sync.dma_start(words[:, cols], y_codes[:, cols].bitcast(I32))
+        scale_rows = out_2.rearrange("z q c -> (z q) c").bitcast(I32)
+        for q in range(4):
+            queue = nc.scalar if q % 2 else nc.sync
+            queue.dma_start(scale_rows[4 * q : 4 * q + 4, :], y_scales[32 * q : 32 * q + 4, :].bitcast(I32))

@@ -19,6 +19,8 @@ P = 128
 PACK = 4
 CHUNK = 256
 X_SPLIT = 340
+W1_SPLIT = 80
+W2_SPLIT = 48
 
 
 def tile_picked_gmem_tanh_lo_kernel(tc, xT, mem, w1, w2, offs, slot, out_0, out_1, out_2):
@@ -31,7 +33,7 @@ def tile_picked_gmem_tanh_lo_kernel(tc, xT, mem, w1, w2, offs, slot, out_0, out_
         slot_t = keep.tile([P, S // 16], U16, name="slot_t")
         x_raw = [keep.tile([P, T], F32, name=f"x_raw{j}") for j in range(PACK)]
         w1_raw = keep.tile([P, PACK, N], F32, name="w1_raw")
-        w2_raw = keep.tile([P, PACK, N], F32, name="w2_raw")
+        w2_raw = keep.tile([P, PACK, N], F32, name="w2_raw", tag="w2_raw")
         page = [keep.tile([P, U], F32, name=f"page{t}") for t in range(PACK)]
 
         x_rows = xT.rearrange("(p j) c -> p j c", j=PACK)
@@ -69,20 +71,21 @@ def tile_picked_gmem_tanh_lo_kernel(tc, xT, mem, w1, w2, offs, slot, out_0, out_
         x_scales = keep.tile([P, S], U8, name="x_scales", align_bytes=64)
         nc.vector.quantize_mx(x_codes[:].bitcast(FP8X4), x_scales[:], x_bf[:].rearrange("p c j -> p (c j)"))
 
-        def deal(copy, raw, t0, t1, name, tag):
-            dealt = keep.tile([P, t1 - t0, P, PACK], BF16, name=name, tag=tag, align_bytes=64)
-            copy(dealt[:].rearrange("p t m j -> p m t j"), raw[:].rearrange("p j (m t) -> p m t j", t=PACK)[:, :, t0:t1, :])
+        def deal(raw, split, name):
+            dealt = keep.tile([P, PACK, P, PACK], BF16, name=name, align_bytes=64)
+            dst = dealt[:].rearrange("p t m j -> p m t j")
+            src = raw[:].rearrange("p j (m t) -> p m t j", t=PACK)
+            nc.scalar.copy(dst[:, :split], src[:, :split])
+            nc.vector.tensor_copy(dst[:, split:], src[:, split:])
             return dealt
 
         stationary = {}
 
-        def quantize_w(which, dealt, first, t0, t1, tag):
+        def quantize_w(which, dealt, t0, t1):
             width = (t1 - t0) * P
-            codes = keep.tile([P, width], U32, name=f"{which}_codes{t0}", tag=tag, align_bytes=64)
+            codes = keep.tile([P, width], U32, name=f"{which}_codes{t0}", align_bytes=64)
             scales = keep.tile([P, width], U8, name=f"{which}_scales{t0}", align_bytes=64)
-            nc.vector.quantize_mx(
-                codes[:].bitcast(FP8X4), scales[:], dealt[:, t0 - first : t1 - first, :, :].rearrange("p t m j -> p (t m j)")
-            )
+            nc.vector.quantize_mx(codes[:].bitcast(FP8X4), scales[:], dealt[:, t0:t1, :, :].rearrange("p t m j -> p (t m j)"))
             for t in range(t0, t1):
                 cols = slice((t - t0) * P, (t - t0 + 1) * P)
                 stationary[which, t] = (codes[:, cols], scales[:, cols])
@@ -101,28 +104,45 @@ def tile_picked_gmem_tanh_lo_kernel(tc, xT, mem, w1, w2, offs, slot, out_0, out_
             )
             return acc
 
-        cand = [keep.tile([P, S], F32, name=f"cand{t}") for t in range(PACK)]
-        stay = [keep.tile([P, S], F32, name=f"stay{t}") for t in range(PACK)]
-        diff = [keep.tile([P, S], F32, name=f"diff{t}", tag="late" if t == 0 else f"diff{t}", align_bytes=64) for t in range(PACK)]
-        kept = [keep.tile([P, S], F32, name=f"kept{t}") for t in range(PACK)]
+        cand = keep.tile([P, PACK, S], F32, name="cand", tag="w2_raw")
+        stay = [keep.tile([P, 2, S], F32, name=f"stay{h}") for h in range(2)]
+        diff = [keep.tile([P, 2, S], F32, name=f"diff{h}") for h in range(2)]
+        kept = [keep.tile([P, 2, S], F32, name=f"kept{h}") for h in range(2)]
+        old = keep.tile([P, 2, S], F32, name="old")
+        new = [keep.tile([P, S], F32, name=f"new{t}") for t in range(PACK)]
         chunks = U // CHUNK
         y_bf = [keep.tile([P, CHUNK, PACK], BF16, name=f"y_bf{c}", align_bytes=64) for c in range(chunks)]
 
         def candidate(t, bank):
-            nc.scalar.activation(cand[t][:], product("w1", t, bank)[:], ACT.Tanh)
+            nc.scalar.activation(cand[:, t, :], product("w1", t, bank)[:], ACT.Tanh)
 
         def gate(t, bank):
-            nc.scalar.activation(stay[t][:], product("w2", t, bank)[:], ACT.Sigmoid, scale=-1.0)
+            nc.scalar.activation(stay[t // 2][:, t % 2, :], product("w2", t, bank)[:], ACT.Sigmoid, scale=-1.0)
 
         def look_up(t):
-            nc.vector.tensor_tensor(diff[t][:], page[t][:].indirect(slot_t[:]), cand[t][:], ALU.subtract)
+            nc.vector.tensor_tensor(diff[t // 2][:, t % 2, :], page[t][:].indirect(slot_t[:]), cand[:, t, :], ALU.subtract)
 
-        def weigh(t):
-            nc.vector.tensor_tensor(kept[t][:], diff[t][:], stay[t][:], ALU.mult)
+        def weigh(t0, t1):
+            h, rows = t0 // 2, slice(t0 % 2, t0 % 2 + t1 - t0)
+            nc.vector.tensor_tensor(kept[h][:, rows, :], diff[h][:, rows, :], stay[h][:, rows, :], ALU.mult)
+
+        def fetch(t):
+            nc.vector.tensor_copy(old[:, t % 2, :], page[t][:].indirect(slot_t[:]))
+
+        def add(t):
+            nc.gpsimd.tensor_tensor(new[t][:], kept[t // 2][:, t % 2, :], cand[:, t, :], ALU.add)
+
+        def blend(t):
+            nc.gpsimd.tensor_tensor(diff[1][:, t % 2, :], old[:, t % 2, :], cand[:, t, :], ALU.subtract)
+            nc.gpsimd.tensor_tensor(kept[1][:, t % 2, :], diff[1][:, t % 2, :], stay[1][:, t % 2, :], ALU.mult)
+            add(t)
 
         def put(t):
-            nc.vector.tensor_tensor(page[t][:].indirect(slot_t[:]), kept[t][:], cand[t][:], ALU.add)
+            nc.vector.tensor_copy(page[t][:].indirect(slot_t[:]), new[t][:])
             nc.sync.dma_start(out_rows[:, t, :], page[t][:])
+            if t + 1 < PACK:
+                for c in range(chunks):
+                    round_out(nc.scalar.copy, t, c)
 
         def round_out(copy, t, c):
             src = page[t][:, c * CHUNK : (c + 1) * CHUNK]
@@ -131,36 +151,31 @@ def tile_picked_gmem_tanh_lo_kernel(tc, xT, mem, w1, w2, offs, slot, out_0, out_
             else:
                 copy(y_bf[c][:, :, t], src)
 
-        w1_first = deal(nc.vector.tensor_copy, w1_raw, 0, 1, "w1_first", "w1_first")
-        w1_rest = deal(nc.scalar.copy, w1_raw, 1, PACK, "w1_rest", "w1_rest")
-        quantize_w("w1", w1_first, 0, 0, 1, "w1_codes0")
+        w1_bf = deal(w1_raw, W1_SPLIT, "w1_bf")
+        quantize_w("w1", w1_bf, 0, 1)
+        quantize_w("w1", w1_bf, 1, 2)
+        quantize_w("w1", w1_bf, 2, 4)
+        w2_bf = deal(w2_raw, W2_SPLIT, "w2_bf")
         candidate(0, "a")
-        quantize_w("w1", w1_rest, 1, 1, 2, "w1_codes1")
-        quantize_w("w1", w1_rest, 1, 2, 4, "w1_codes2")
-        w2_first = deal(nc.vector.tensor_copy, w2_raw, 0, 1, "w2_first", "w2_first")
-        w2_mid = deal(nc.scalar.copy, w2_raw, 1, 3, "w2_mid", "w2_mid")
-        quantize_w("w2", w2_first, 0, 0, 1, "w2_codes0")
-        gate(0, "b")
+        candidate(1, "b")
+        quantize_w("w2", w2_bf, 0, PACK)
+        gate(0, "c")
+        gate(1, "d")
+        candidate(2, "e")
+        candidate(3, "d")
+        gate(2, "c")
+        gate(3, "c")
         look_up(0)
-        candidate(1, "c")
-        candidate(2, "b")
-        candidate(3, "b")
+        look_up(1)
+        weigh(0, 2)
+        add(0)
+        add(1)
+        fetch(2)
+        fetch(3)
+        blend(2)
+        blend(3)
         for t in range(PACK):
-            weigh(t)
-            if t + 1 < PACK:
-                look_up(t + 1)
-            if t == 0:
-                quantize_w("w2", w2_mid, 1, 1, 3, "late")
-                gate(1, "a")
-                gate(2, "a")
-                w2_last = deal(nc.scalar.copy, w2_raw, 3, 4, "w2_last", "late")
-            if t == 1:
-                quantize_w("w2", w2_last, 3, 3, 4, "w2_codes3")
-                gate(3, "a")
             put(t)
-            if t + 1 < PACK:
-                for c in range(chunks):
-                    round_out(nc.scalar.copy, t, c)
 
         y_codes = keep.tile([P, U], U32, name="y_codes", align_bytes=64)
         y_scales = keep.tile([P, U], U8, name="y_scales", align_bytes=64)

@@ -17,7 +17,7 @@ ACT = mybir.ActivationFunctionType
 
 P = 128
 PACK = 4
-CHUNK = 256
+SHARES = ((0, 512), (512, 768), (768, 1024))
 X_SPLIT = 340
 W1_SPLIT = 80
 W2_SPLIT = 48
@@ -105,51 +105,53 @@ def tile_picked_gmem_tanh_lo_kernel(tc, xT, mem, w1, w2, offs, slot, out_0, out_
             return acc
 
         cand = keep.tile([P, PACK, S], F32, name="cand", tag="w2_raw")
-        stay = [keep.tile([P, 2, S], F32, name=f"stay{h}") for h in range(2)]
-        diff = [keep.tile([P, 2, S], F32, name=f"diff{h}") for h in range(2)]
-        kept = [keep.tile([P, 2, S], F32, name=f"kept{h}") for h in range(2)]
-        old = keep.tile([P, 2, S], F32, name="old")
-        new = [keep.tile([P, S], F32, name=f"new{t}") for t in range(PACK)]
-        chunks = U // CHUNK
-        y_bf = [keep.tile([P, CHUNK, PACK], BF16, name=f"y_bf{c}", align_bytes=64) for c in range(chunks)]
+        stay = [keep.tile([P, S], F32, name=f"stay{t}") for t in range(PACK)]
+        diff, kept = {}, {}
+        new = [keep.tile([P, S], F32, name=f"new{t}") for t in range(PACK - 1)]
+        old = {t: keep.tile([P, S], F32, name=f"old{t}") for t in range(2, PACK)}
+        y_bf = [keep.tile([P, hi - lo, PACK], BF16, name=f"y_bf{lo}", align_bytes=64) for lo, hi in SHARES]
 
         def candidate(t, bank):
             nc.scalar.activation(cand[:, t, :], product("w1", t, bank)[:], ACT.Tanh)
 
         def gate(t, bank):
-            nc.scalar.activation(stay[t // 2][:, t % 2, :], product("w2", t, bank)[:], ACT.Sigmoid, scale=-1.0)
+            nc.scalar.activation(stay[t][:], product("w2", t, bank)[:], ACT.Sigmoid, scale=-1.0)
 
         def look_up(t):
-            nc.vector.tensor_tensor(diff[t // 2][:, t % 2, :], page[t][:].indirect(slot_t[:]), cand[:, t, :], ALU.subtract)
-
-        def weigh(t0, t1):
-            h, rows = t0 // 2, slice(t0 % 2, t0 % 2 + t1 - t0)
-            nc.vector.tensor_tensor(kept[h][:, rows, :], diff[h][:, rows, :], stay[h][:, rows, :], ALU.mult)
+            diff[t] = keep.tile([P, S], F32, name=f"diff{t}")
+            nc.vector.tensor_tensor(diff[t][:], page[t][:].indirect(slot_t[:]), cand[:, t, :], ALU.subtract)
 
         def fetch(t):
-            nc.vector.tensor_copy(old[:, t % 2, :], page[t][:].indirect(slot_t[:]))
+            nc.vector.tensor_copy(old[t][:], page[t][:].indirect(slot_t[:]))
+
+        def subtract(t):
+            diff[t] = keep.tile([P, S], F32, name=f"diff{t}", tag=f"turn{t % 2}")
+            nc.gpsimd.tensor_tensor(diff[t][:], old[t][:], cand[:, t, :], ALU.subtract)
+
+        def weigh(engine, t):
+            kept[t] = keep.tile([P, S], F32, name=f"kept{t}", tag=f"turn{max(t - 1, 0) % 2}")
+            engine.tensor_tensor(kept[t][:], diff[t][:], stay[t][:], ALU.mult)
 
         def add(t):
-            nc.gpsimd.tensor_tensor(new[t][:], kept[t // 2][:, t % 2, :], cand[:, t, :], ALU.add)
-
-        def blend(t):
-            nc.gpsimd.tensor_tensor(diff[1][:, t % 2, :], old[:, t % 2, :], cand[:, t, :], ALU.subtract)
-            nc.gpsimd.tensor_tensor(kept[1][:, t % 2, :], diff[1][:, t % 2, :], stay[1][:, t % 2, :], ALU.mult)
-            add(t)
-
-        def put(t):
-            nc.vector.tensor_copy(page[t][:].indirect(slot_t[:]), new[t][:])
-            nc.sync.dma_start(out_rows[:, t, :], page[t][:])
-            if t + 1 < PACK:
-                for c in range(chunks):
-                    round_out(nc.scalar.copy, t, c)
+            nc.gpsimd.tensor_tensor(new[t][:], kept[t][:], cand[:, t, :], ALU.add)
 
         def round_out(copy, t, c):
-            src = page[t][:, c * CHUNK : (c + 1) * CHUNK]
-            if t == 2 and c % 2 == 0:
-                copy(y_bf[c][:, :, 2:4], src.unsqueeze(2).to_broadcast([P, CHUNK, 2]))
+            lo, hi = SHARES[c]
+            src = page[t][:, lo:hi]
+            if t == 2 and c == 0:
+                copy(y_bf[c][:, :, 2:4], src.unsqueeze(2).to_broadcast([P, hi - lo, 2]))
             else:
                 copy(y_bf[c][:, :, t], src)
+
+        def put(t):
+            if t + 1 < PACK:
+                nc.vector.tensor_copy(page[t][:].indirect(slot_t[:]), new[t][:])
+            else:
+                nc.vector.tensor_tensor(page[t][:].indirect(slot_t[:]), kept[t][:], cand[:, t, :], ALU.add)
+            nc.sync.dma_start(out_rows[:, t, :], page[t][:])
+            if t + 1 < PACK:
+                for c in range(len(SHARES)):
+                    round_out(nc.scalar.copy, t, c)
 
         w1_bf = deal(w1_raw, W1_SPLIT, "w1_bf")
         quantize_w("w1", w1_bf, 0, 1)
@@ -167,13 +169,16 @@ def tile_picked_gmem_tanh_lo_kernel(tc, xT, mem, w1, w2, offs, slot, out_0, out_
         gate(3, "c")
         look_up(0)
         look_up(1)
-        weigh(0, 2)
+        weigh(nc.vector, 0)
         add(0)
+        weigh(nc.gpsimd, 1)
         add(1)
-        fetch(2)
-        fetch(3)
-        blend(2)
-        blend(3)
+        for t in range(2, PACK):
+            fetch(t)
+            subtract(t)
+            weigh(nc.gpsimd, t)
+            if t + 1 < PACK:
+                add(t)
         for t in range(PACK):
             put(t)
 
@@ -181,10 +186,10 @@ def tile_picked_gmem_tanh_lo_kernel(tc, xT, mem, w1, w2, offs, slot, out_0, out_
         y_scales = keep.tile([P, U], U8, name="y_scales", align_bytes=64)
         words = out_1.rearrange("z l c r -> (z l) (c r)").bitcast(I32)
         last = PACK - 1
-        for c in range(chunks):
-            round_out(nc.scalar.copy if c % 2 else nc.vector.tensor_copy, last, c)
-        for c in range(chunks):
-            cols = slice(c * CHUNK, (c + 1) * CHUNK)
+        for c in range(len(SHARES)):
+            round_out(nc.scalar.copy if c else nc.vector.tensor_copy, last, c)
+        for c, (lo, hi) in enumerate(SHARES):
+            cols = slice(lo, hi)
             nc.vector.quantize_mx(y_codes[:, cols].bitcast(FP8X4), y_scales[:, cols], y_bf[c][:].rearrange("p c r -> p (c r)"))
             nc.sync.dma_start(words[:, cols], y_codes[:, cols].bitcast(I32))
         scale_rows = out_2.rearrange("z q c -> (z q) c").bitcast(I32)

@@ -18,9 +18,8 @@ ACT = mybir.ActivationFunctionType
 P = 128
 PACK = 4
 SHARES = ((0, 512), (512, 768), (768, 1024))
-X_SPLIT = 340
-W1_SPLIT = 80
-W2_SPLIT = 48
+HALF = N // 2
+LAP = 0
 
 
 def tile_picked_gmem_tanh_lo_kernel(tc, xT, mem, w1, w2, offs, slot, out_0, out_1, out_2):
@@ -32,8 +31,7 @@ def tile_picked_gmem_tanh_lo_kernel(tc, xT, mem, w1, w2, offs, slot, out_0, out_
         offs_t = keep.tile([P, S // 16], U16, name="offs_t")
         slot_t = keep.tile([P, S // 16], U16, name="slot_t")
         x_raw = [keep.tile([P, T], F32, name=f"x_raw{j}") for j in range(PACK)]
-        w1_raw = keep.tile([P, PACK, N], F32, name="w1_raw")
-        w2_raw = keep.tile([P, PACK, N], F32, name="w2_raw", tag="w2_raw")
+        w_raw = {(w, h): keep.tile([P, PACK, HALF], F32, name=f"{w}_raw{h}") for w in ("w1", "w2") for h in range(2)}
         page = [keep.tile([P, U], F32, name=f"page{t}") for t in range(PACK)]
 
         x_rows = xT.rearrange("(p j) c -> p j c", j=PACK)
@@ -43,8 +41,10 @@ def tile_picked_gmem_tanh_lo_kernel(tc, xT, mem, w1, w2, offs, slot, out_0, out_
         nc.sync.dma_start(offs_t[:], offs)
         for j in range(PACK):
             nc.sync.dma_start(x_raw[j][:], x_rows[:, j, :])
-        nc.sync.dma_start(w1_raw[:], w1.rearrange("(p j) c -> p j c", j=PACK))
-        nc.sync.dma_start(w2_raw[:], w2.rearrange("(p j) c -> p j c", j=PACK))
+        for name, w in (("w1", w1), ("w2", w2)):
+            rows = w.rearrange("(p j) c -> p j c", j=PACK)
+            for h in range(2):
+                nc.sync.dma_start(w_raw[name, h][:], rows[:, :, h * HALF : (h + 1) * HALF])
         nc.sync.dma_start(slot_t[:], slot)
         for t in range(PACK):
             nc.sync.dma_start(page[t][:], mem_rows[:, t, :])
@@ -64,20 +64,18 @@ def tile_picked_gmem_tanh_lo_kernel(tc, xT, mem, w1, w2, offs, slot, out_0, out_
             nc.vector.tensor_copy(picked[j // 2][:, j % 2, :], x_raw[j][:].indirect(offs_t[:]))
             if j == 1:
                 weave_x(nc.scalar.copy, 0, 0, S)
-        weave_x(nc.vector.tensor_copy, 1, 0, X_SPLIT)
-        weave_x(nc.scalar.copy, 1, X_SPLIT, S)
+        weave_x(nc.vector.tensor_copy, 1, 0, S)
 
         x_codes = keep.tile([P, S], U32, name="x_codes", align_bytes=64)
         x_scales = keep.tile([P, S], U8, name="x_scales", align_bytes=64)
         nc.vector.quantize_mx(x_codes[:].bitcast(FP8X4), x_scales[:], x_bf[:].rearrange("p c j -> p (c j)"))
 
-        def deal(raw, split, name):
-            dealt = keep.tile([P, PACK, P, PACK], BF16, name=name, align_bytes=64)
-            dst = dealt[:].rearrange("p t m j -> p m t j")
-            src = raw[:].rearrange("p j (m t) -> p m t j", t=PACK)
-            nc.scalar.copy(dst[:, :split], src[:, :split])
-            nc.vector.tensor_copy(dst[:, split:], src[:, split:])
-            return dealt
+        w_bf = {w: keep.tile([P, PACK, P, PACK], BF16, name=f"{w}_bf", align_bytes=64) for w in ("w1", "w2")}
+
+        def deal(copy, which, h):
+            dst = w_bf[which][:].rearrange("p t m j -> p m j t")
+            src = w_raw[which, h][:].rearrange("p j (m t) -> p m j t", t=PACK)
+            copy(dst[:, h * (P // 2) : (h + 1) * (P // 2)], src)
 
         stationary = {}
 
@@ -104,81 +102,89 @@ def tile_picked_gmem_tanh_lo_kernel(tc, xT, mem, w1, w2, offs, slot, out_0, out_
             )
             return acc
 
-        cand = keep.tile([P, PACK, S], F32, name="cand", tag="w2_raw")
-        stay = [keep.tile([P, S], F32, name=f"stay{t}") for t in range(PACK)]
-        diff, kept = {}, {}
-        new = [keep.tile([P, S], F32, name=f"new{t}") for t in range(PACK - 1)]
+        cand = keep.tile([P, PACK, S], F32, name="cand")
+        stay_all = keep.tile([P, PACK * S], F32, name="stay_all")
+        stay = [stay_all[:, t * S : (t + 1) * S] for t in range(PACK)]
+        diff01 = keep.tile([P, 2 * S], F32, name="diff01")
+        diff = {t: diff01[:, t * S : (t + 1) * S] for t in range(2)}
+        kept = {}
+        cand_all = cand[:].rearrange("p t s -> p (t s)")
+        new_all = keep.tile([P, (PACK - 1) * S], F32, name="new_all")
+        new = [new_all[:, t * S : (t + 1) * S] for t in range(PACK - 1)]
         old = {t: keep.tile([P, S], F32, name=f"old{t}") for t in range(2, PACK)}
-        y_bf = [keep.tile([P, hi - lo, PACK], BF16, name=f"y_bf{lo}", align_bytes=64) for lo, hi in SHARES]
+        y_bf = keep.tile([P, U, PACK], BF16, name="y_bf", align_bytes=64)
 
         def candidate(t, bank):
             nc.scalar.activation(cand[:, t, :], product("w1", t, bank)[:], ACT.Tanh)
 
         def gate(t, bank):
-            nc.scalar.activation(stay[t][:], product("w2", t, bank)[:], ACT.Sigmoid, scale=-1.0)
+            nc.scalar.activation(stay[t], product("w2", t, bank)[:], ACT.Sigmoid, scale=-1.0)
 
         def look_up(t):
-            diff[t] = keep.tile([P, S], F32, name=f"diff{t}")
-            nc.vector.tensor_tensor(diff[t][:], page[t][:].indirect(slot_t[:]), cand[:, t, :], ALU.subtract)
+            nc.vector.tensor_tensor(diff[t], page[t][:].indirect(slot_t[:]), cand[:, t, :], ALU.subtract)
 
         def fetch(t):
             nc.vector.tensor_copy(old[t][:], page[t][:].indirect(slot_t[:]))
 
         def subtract(t):
-            diff[t] = keep.tile([P, S], F32, name=f"diff{t}", tag=f"turn{t % 2}")
-            nc.gpsimd.tensor_tensor(diff[t][:], old[t][:], cand[:, t, :], ALU.subtract)
+            diff[t] = keep.tile([P, S], F32, name=f"diff{t}", tag=f"turn{t % 2}")[:]
+            nc.gpsimd.tensor_tensor(diff[t], old[t][:], cand[:, t, :], ALU.subtract)
+
+        def blend_first(engine, lo, hi):
+            part = keep.tile([P, hi - lo], F32, name=f"kept_from{lo}", tag="turn0")
+            engine.tensor_tensor(part[:], diff01[:, lo:hi], stay_all[:, lo:hi], ALU.mult)
+            nc.gpsimd.tensor_tensor(new_all[:, lo:hi], part[:], cand_all[:, lo:hi], ALU.add)
 
         def weigh(engine, t):
-            kept[t] = keep.tile([P, S], F32, name=f"kept{t}", tag=f"turn{max(t - 1, 0) % 2}")
-            engine.tensor_tensor(kept[t][:], diff[t][:], stay[t][:], ALU.mult)
+            kept[t] = keep.tile([P, S], F32, name=f"kept{t}", tag=f"turn{(t - 1) % 2}")[:]
+            engine.tensor_tensor(kept[t], diff[t], stay[t], ALU.mult)
 
         def add(t):
-            nc.gpsimd.tensor_tensor(new[t][:], kept[t][:], cand[:, t, :], ALU.add)
+            nc.gpsimd.tensor_tensor(new[t], kept[t], cand[:, t, :], ALU.add)
 
-        def round_out(copy, t, c):
-            lo, hi = SHARES[c]
-            src = page[t][:, lo:hi]
-            if t == 2 and c == 0:
-                copy(y_bf[c][:, :, 2:4], src.unsqueeze(2).to_broadcast([P, hi - lo, 2]))
-            else:
-                copy(y_bf[c][:, :, t], src)
+        def round_out(copy, t, lo, hi):
+            copy(y_bf[:, lo:hi, t], page[t][:, lo:hi])
 
         def put(t):
             if t + 1 < PACK:
-                nc.vector.tensor_copy(page[t][:].indirect(slot_t[:]), new[t][:])
+                nc.vector.tensor_copy(page[t][:].indirect(slot_t[:]), new[t])
             else:
-                nc.vector.tensor_tensor(page[t][:].indirect(slot_t[:]), kept[t][:], cand[:, t, :], ALU.add)
+                nc.vector.tensor_tensor(page[t][:].indirect(slot_t[:]), kept[t], cand[:, t, :], ALU.add)
             nc.sync.dma_start(out_rows[:, t, :], page[t][:])
-            if t + 1 < PACK:
-                for c in range(len(SHARES)):
-                    round_out(nc.scalar.copy, t, c)
+            if t < 2:
+                round_out(nc.scalar.copy, t, 0, U)
+            elif t == 2:
+                lo, hi = SHARES[0]
+                nc.scalar.copy(y_bf[:, lo:hi, 2:4], page[t][:, lo:hi].unsqueeze(2).to_broadcast([P, hi - lo, 2]))
+                round_out(nc.scalar.copy, t, hi, U)
 
-        w1_bf = deal(w1_raw, W1_SPLIT, "w1_bf")
-        quantize_w("w1", w1_bf, 0, 1)
-        quantize_w("w1", w1_bf, 1, 2)
-        quantize_w("w1", w1_bf, 2, 4)
-        w2_bf = deal(w2_raw, W2_SPLIT, "w2_bf")
+        deal(nc.scalar.copy, "w1", 0)
+        deal(nc.scalar.copy, "w1", 1)
+        quantize_w("w1", w_bf["w1"], 0, 1)
+        quantize_w("w1", w_bf["w1"], 1, 2)
+        quantize_w("w1", w_bf["w1"], 2, 4)
+        deal(nc.scalar.copy, "w2", 0)
+        deal(nc.vector.tensor_copy, "w2", 1)
         candidate(0, "a")
+        quantize_w("w2", w_bf["w2"], 0, PACK)
         candidate(1, "b")
-        quantize_w("w2", w2_bf, 0, PACK)
-        gate(0, "c")
-        gate(1, "d")
         candidate(2, "e")
-        candidate(3, "d")
-        gate(2, "c")
-        gate(3, "c")
+        candidate(3, "f")
+        gate(0, "e")
+        gate(1, "d")
+        gate(2, "g")
+        gate(3, "h")
         look_up(0)
         look_up(1)
-        weigh(nc.vector, 0)
-        add(0)
-        weigh(nc.gpsimd, 1)
-        add(1)
-        for t in range(2, PACK):
-            fetch(t)
-            subtract(t)
-            weigh(nc.gpsimd, t)
-            if t + 1 < PACK:
-                add(t)
+        blend_first(nc.vector, 0, S + LAP)
+        fetch(2)
+        fetch(3)
+        blend_first(nc.gpsimd, S + LAP, 2 * S)
+        subtract(2)
+        weigh(nc.gpsimd, 2)
+        add(2)
+        subtract(3)
+        weigh(nc.gpsimd, 3)
         for t in range(PACK):
             put(t)
 
@@ -187,10 +193,10 @@ def tile_picked_gmem_tanh_lo_kernel(tc, xT, mem, w1, w2, offs, slot, out_0, out_
         words = out_1.rearrange("z l c r -> (z l) (c r)").bitcast(I32)
         last = PACK - 1
         for c in range(len(SHARES)):
-            round_out(nc.scalar.copy if c else nc.vector.tensor_copy, last, c)
-        for c, (lo, hi) in enumerate(SHARES):
-            cols = slice(lo, hi)
-            nc.vector.quantize_mx(y_codes[:, cols].bitcast(FP8X4), y_scales[:, cols], y_bf[c][:].rearrange("p c r -> p (c r)"))
+            round_out(nc.scalar.copy if c else nc.vector.tensor_copy, last, *SHARES[c])
+        for c in (1, 0, 2):
+            cols = slice(*SHARES[c])
+            nc.vector.quantize_mx(y_codes[:, cols].bitcast(FP8X4), y_scales[:, cols], y_bf[:, cols, :].rearrange("p c r -> p (c r)"))
             nc.sync.dma_start(words[:, cols], y_codes[:, cols].bitcast(I32))
         scale_rows = out_2.rearrange("z q c -> (z q) c").bitcast(I32)
         for q in range(4):

@@ -32,21 +32,22 @@ def tile_picked_gmem_tanh_lo_kernel(tc, xT, mem, w1, w2, offs, slot, out_0, out_
         slot_t = keep.tile([P, S // 16], U16, name="slot_t")
         x_raw = [keep.tile([P, T], F32, name=f"x_raw{j}") for j in range(PACK)]
         w_raw = {(w, h): keep.tile([P, PACK, HALF], F32, name=f"{w}_raw{h}") for w in ("w1", "w2") for h in range(2)}
-        page = [keep.tile([P, U], F32, name=f"page{t}") for t in range(PACK)]
+        page = [keep.tile([P, U], F32, name=f"page{t}") for t in range(PACK - 1)]
 
         x_rows = xT.rearrange("(p j) c -> p j c", j=PACK)
         mem_rows = mem.rearrange("(p t) c -> p t c", t=PACK)
         out_rows = out_0.rearrange("(p t) c -> p t c", t=PACK)
 
-        nc.sync.dma_start(offs_t[:], offs)
         for j in range(PACK):
             nc.sync.dma_start(x_raw[j][:], x_rows[:, j, :])
+            if j == 0:
+                nc.sync.dma_start(offs_t[:], offs)
         for name, w in (("w1", w1), ("w2", w2)):
             rows = w.rearrange("(p j) c -> p j c", j=PACK)
             for h in range(2):
                 nc.sync.dma_start(w_raw[name, h][:], rows[:, :, h * HALF : (h + 1) * HALF])
         nc.sync.dma_start(slot_t[:], slot)
-        for t in range(PACK):
+        for t in range(PACK - 1):
             nc.sync.dma_start(page[t][:], mem_rows[:, t, :])
 
         warm_in = keep.tile([P, 1], F32, name="warm_in")
@@ -70,7 +71,7 @@ def tile_picked_gmem_tanh_lo_kernel(tc, xT, mem, w1, w2, offs, slot, out_0, out_
         x_scales = keep.tile([P, S], U8, name="x_scales", align_bytes=64)
         nc.vector.quantize_mx(x_codes[:].bitcast(FP8X4), x_scales[:], x_bf[:].rearrange("p c j -> p (c j)"))
 
-        w_bf = {w: keep.tile([P, PACK, P, PACK], BF16, name=f"{w}_bf", align_bytes=64) for w in ("w1", "w2")}
+        w_bf = {w: keep.tile([P, PACK, P, PACK], BF16, name=f"{w}_bf", tag=f"{w}_bf", align_bytes=64) for w in ("w1", "w2")}
 
         def deal(copy, which, h):
             dst = w_bf[which][:].rearrange("p t m j -> p m j t")
@@ -167,6 +168,8 @@ def tile_picked_gmem_tanh_lo_kernel(tc, xT, mem, w1, w2, offs, slot, out_0, out_
         deal(nc.vector.tensor_copy, "w2", 1)
         candidate(0, "a")
         quantize_w("w2", w_bf["w2"], 0, PACK)
+        page.append(keep.tile([P, U], F32, name="page3", tag="w2_bf", align_bytes=64))
+        nc.scalar.dma_start(page[3][:], mem_rows[:, 3, :])
         candidate(1, "b")
         candidate(2, "e")
         candidate(3, "f")

@@ -17,9 +17,9 @@ ACT = mybir.ActivationFunctionType
 
 P = 128
 PACK = 4
-SHARES = ((0, 512), (512, 768), (768, 1024))
+LAST = PACK - 1
 HALF = N // 2
-LAP = 0
+SHARES = ((0, 512), (512, 768), (768, 1024))
 
 
 def tile_picked_gmem_tanh_lo_kernel(tc, xT, mem, w1, w2, offs, slot, out_0, out_1, out_2):
@@ -32,7 +32,7 @@ def tile_picked_gmem_tanh_lo_kernel(tc, xT, mem, w1, w2, offs, slot, out_0, out_
         slot_t = keep.tile([P, S // 16], U16, name="slot_t")
         x_raw = [keep.tile([P, T], F32, name=f"x_raw{j}") for j in range(PACK)]
         w_raw = {(w, h): keep.tile([P, PACK, HALF], F32, name=f"{w}_raw{h}") for w in ("w1", "w2") for h in range(2)}
-        page = [keep.tile([P, U], F32, name=f"page{t}") for t in range(PACK - 1)]
+        page = [keep.tile([P, U], F32, name=f"page{t}") for t in range(LAST)]
 
         x_rows = xT.rearrange("(p j) c -> p j c", j=PACK)
         mem_rows = mem.rearrange("(p t) c -> p t c", t=PACK)
@@ -42,12 +42,12 @@ def tile_picked_gmem_tanh_lo_kernel(tc, xT, mem, w1, w2, offs, slot, out_0, out_
             nc.sync.dma_start(x_raw[j][:], x_rows[:, j, :])
             if j == 0:
                 nc.sync.dma_start(offs_t[:], offs)
-        for name, w in (("w1", w1), ("w2", w2)):
-            rows = w.rearrange("(p j) c -> p j c", j=PACK)
+        for which, w in (("w1", w1), ("w2", w2)):
+            w_rows = w.rearrange("(p j) c -> p j c", j=PACK)
             for h in range(2):
-                nc.sync.dma_start(w_raw[name, h][:], rows[:, :, h * HALF : (h + 1) * HALF])
+                nc.sync.dma_start(w_raw[which, h][:], w_rows[:, :, h * HALF : (h + 1) * HALF])
         nc.sync.dma_start(slot_t[:], slot)
-        for t in range(PACK - 1):
+        for t in range(LAST):
             nc.sync.dma_start(page[t][:], mem_rows[:, t, :])
 
         warm_in = keep.tile([P, 1], F32, name="warm_in")
@@ -55,17 +55,17 @@ def tile_picked_gmem_tanh_lo_kernel(tc, xT, mem, w1, w2, offs, slot, out_0, out_
         nc.gpsimd.memset(warm_in[:], 0.0)
         nc.scalar.activation(warm_out[:], warm_in[:], ACT.Sigmoid)
 
-        picked = [keep.tile([P, 2, S], F32, name=f"picked{h}") for h in range(2)]
+        picked = [keep.tile([P, 2, S], F32, name=f"picked{pair}") for pair in range(2)]
         x_bf = keep.tile([P, S, PACK], BF16, name="x_bf", align_bytes=64)
 
-        def weave_x(copy, h, lo, hi):
-            copy(x_bf[:, lo:hi, 2 * h : 2 * h + 2], picked[h][:, :, lo:hi].rearrange("p e c -> p c e"))
+        def interleave_x(copy, pair):
+            copy(x_bf[:, :, 2 * pair : 2 * pair + 2], picked[pair][:].rearrange("p e c -> p c e"))
 
         for j in range(PACK):
             nc.vector.tensor_copy(picked[j // 2][:, j % 2, :], x_raw[j][:].indirect(offs_t[:]))
             if j == 1:
-                weave_x(nc.scalar.copy, 0, 0, S)
-        weave_x(nc.vector.tensor_copy, 1, 0, S)
+                interleave_x(nc.scalar.copy, 0)
+        interleave_x(nc.vector.tensor_copy, 1)
 
         x_codes = keep.tile([P, S], U32, name="x_codes", align_bytes=64)
         x_scales = keep.tile([P, S], U8, name="x_scales", align_bytes=64)
@@ -73,18 +73,18 @@ def tile_picked_gmem_tanh_lo_kernel(tc, xT, mem, w1, w2, offs, slot, out_0, out_
 
         w_bf = {w: keep.tile([P, PACK, P, PACK], BF16, name=f"{w}_bf", tag=f"{w}_bf", align_bytes=64) for w in ("w1", "w2")}
 
-        def deal(copy, which, h):
+        def regroup_w(copy, which, h):
             dst = w_bf[which][:].rearrange("p t m j -> p m j t")
             src = w_raw[which, h][:].rearrange("p j (m t) -> p m j t", t=PACK)
             copy(dst[:, h * (P // 2) : (h + 1) * (P // 2)], src)
 
         stationary = {}
 
-        def quantize_w(which, dealt, t0, t1):
+        def quantize_w(which, t0, t1):
             width = (t1 - t0) * P
             codes = keep.tile([P, width], U32, name=f"{which}_codes{t0}", align_bytes=64)
             scales = keep.tile([P, width], U8, name=f"{which}_scales{t0}", align_bytes=64)
-            nc.vector.quantize_mx(codes[:].bitcast(FP8X4), scales[:], dealt[:, t0:t1, :, :].rearrange("p t m j -> p (t m j)"))
+            nc.vector.quantize_mx(codes[:].bitcast(FP8X4), scales[:], w_bf[which][:, t0:t1, :, :].rearrange("p t m j -> p (t m j)"))
             for t in range(t0, t1):
                 cols = slice((t - t0) * P, (t - t0 + 1) * P)
                 stationary[which, t] = (codes[:, cols], scales[:, cols])
@@ -104,14 +104,11 @@ def tile_picked_gmem_tanh_lo_kernel(tc, xT, mem, w1, w2, offs, slot, out_0, out_
             return acc
 
         cand = keep.tile([P, PACK, S], F32, name="cand")
-        stay_all = keep.tile([P, PACK * S], F32, name="stay_all")
-        stay = [stay_all[:, t * S : (t + 1) * S] for t in range(PACK)]
-        diff01 = keep.tile([P, 2 * S], F32, name="diff01")
-        diff = {t: diff01[:, t * S : (t + 1) * S] for t in range(2)}
+        stay = keep.tile([P, PACK, S], F32, name="stay")
+        diff_fused = keep.tile([P, 2, S], F32, name="diff_fused")
+        diff = {t: diff_fused[:, t, :] for t in range(2)}
         kept = {}
-        cand_all = cand[:].rearrange("p t s -> p (t s)")
-        new_all = keep.tile([P, (PACK - 1) * S], F32, name="new_all")
-        new = [new_all[:, t * S : (t + 1) * S] for t in range(PACK - 1)]
+        new = keep.tile([P, LAST, S], F32, name="new")
         old = {t: keep.tile([P, S], F32, name=f"old{t}") for t in range(2, PACK)}
         y_bf = keep.tile([P, U, PACK], BF16, name="y_bf", align_bytes=64)
 
@@ -119,89 +116,88 @@ def tile_picked_gmem_tanh_lo_kernel(tc, xT, mem, w1, w2, offs, slot, out_0, out_
             nc.scalar.activation(cand[:, t, :], product("w1", t, bank)[:], ACT.Tanh)
 
         def gate(t, bank):
-            nc.scalar.activation(stay[t], product("w2", t, bank)[:], ACT.Sigmoid, scale=-1.0)
+            nc.scalar.activation(stay[:, t, :], product("w2", t, bank)[:], ACT.Sigmoid, scale=-1.0)
 
-        def look_up(t):
+        def gather_and_subtract(t):
             nc.vector.tensor_tensor(diff[t], page[t][:].indirect(slot_t[:]), cand[:, t, :], ALU.subtract)
 
-        def fetch(t):
+        def gather(t):
             nc.vector.tensor_copy(old[t][:], page[t][:].indirect(slot_t[:]))
 
-        def subtract(t):
-            diff[t] = keep.tile([P, S], F32, name=f"diff{t}", tag=f"turn{t % 2}")[:]
+        def subtract(t, scratch):
+            diff[t] = keep.tile([P, S], F32, name=f"diff{t}", tag=scratch)[:]
             nc.gpsimd.tensor_tensor(diff[t], old[t][:], cand[:, t, :], ALU.subtract)
 
-        def blend_first(engine, lo, hi):
-            part = keep.tile([P, hi - lo], F32, name=f"kept_from{lo}", tag="turn0")
-            engine.tensor_tensor(part[:], diff01[:, lo:hi], stay_all[:, lo:hi], ALU.mult)
-            nc.gpsimd.tensor_tensor(new_all[:, lo:hi], part[:], cand_all[:, lo:hi], ALU.add)
-
-        def weigh(engine, t):
-            kept[t] = keep.tile([P, S], F32, name=f"kept{t}", tag=f"turn{(t - 1) % 2}")[:]
-            engine.tensor_tensor(kept[t], diff[t], stay[t], ALU.mult)
+        def weigh(engine, t, scratch):
+            kept[t] = keep.tile([P, S], F32, name=f"kept{t}", tag=scratch)[:]
+            engine.tensor_tensor(kept[t], diff[t], stay[:, t, :], ALU.mult)
 
         def add(t):
-            nc.gpsimd.tensor_tensor(new[t], kept[t], cand[:, t, :], ALU.add)
+            nc.gpsimd.tensor_tensor(new[:, t, :], kept[t], cand[:, t, :], ALU.add)
 
         def round_out(copy, t, lo, hi):
             copy(y_bf[:, lo:hi, t], page[t][:, lo:hi])
 
-        def put(t):
-            if t + 1 < PACK:
-                nc.vector.tensor_copy(page[t][:].indirect(slot_t[:]), new[t])
+        def scatter_and_store(t):
+            if t < LAST:
+                nc.vector.tensor_copy(page[t][:].indirect(slot_t[:]), new[:, t, :])
             else:
                 nc.vector.tensor_tensor(page[t][:].indirect(slot_t[:]), kept[t], cand[:, t, :], ALU.add)
             nc.sync.dma_start(out_rows[:, t, :], page[t][:])
-            if t < 2:
+            if t < LAST - 1:
                 round_out(nc.scalar.copy, t, 0, U)
-            elif t == 2:
+            elif t == LAST - 1:
                 lo, hi = SHARES[0]
                 nc.scalar.copy(y_bf[:, lo:hi, 2:4], page[t][:, lo:hi].unsqueeze(2).to_broadcast([P, hi - lo, 2]))
                 round_out(nc.scalar.copy, t, hi, U)
 
-        deal(nc.scalar.copy, "w1", 0)
-        deal(nc.scalar.copy, "w1", 1)
-        quantize_w("w1", w_bf["w1"], 0, 1)
-        quantize_w("w1", w_bf["w1"], 1, 2)
-        quantize_w("w1", w_bf["w1"], 2, 4)
-        deal(nc.scalar.copy, "w2", 0)
-        deal(nc.vector.tensor_copy, "w2", 1)
-        candidate(0, "a")
-        quantize_w("w2", w_bf["w2"], 0, PACK)
-        page.append(keep.tile([P, U], F32, name="page3", tag="w2_bf", align_bytes=64))
-        nc.scalar.dma_start(page[3][:], mem_rows[:, 3, :])
-        candidate(1, "b")
-        candidate(2, "e")
-        candidate(3, "f")
-        gate(0, "e")
-        gate(1, "d")
-        gate(2, "g")
-        gate(3, "h")
-        look_up(0)
-        look_up(1)
-        blend_first(nc.vector, 0, S + LAP)
-        fetch(2)
-        fetch(3)
-        blend_first(nc.gpsimd, S + LAP, 2 * S)
-        subtract(2)
-        weigh(nc.gpsimd, 2)
+        regroup_w(nc.scalar.copy, "w1", 0)
+        regroup_w(nc.scalar.copy, "w1", 1)
+        quantize_w("w1", 0, 1)
+        quantize_w("w1", 1, 2)
+        quantize_w("w1", 2, PACK)
+        regroup_w(nc.scalar.copy, "w2", 0)
+        regroup_w(nc.vector.tensor_copy, "w2", 1)
+        candidate(0, "bank0")
+        quantize_w("w2", 0, PACK)
+
+        page.append(keep.tile([P, U], F32, name=f"page{LAST}", tag="w2_bf", align_bytes=64))
+        nc.scalar.dma_start(page[LAST][:], mem_rows[:, LAST, :])
+
+        candidate(1, "bank1")
+        candidate(2, "bank2")
+        gate(0, "bank1")
+        candidate(3, "bank3")
+        gate(1, "bank4")
+        gate(2, "bank5")
+        gate(3, "bank6")
+
+        gather_and_subtract(0)
+        gather_and_subtract(1)
+        weigh(nc.vector, 0, "scratch0")
+        add(0)
+        gather(2)
+        gather(3)
+        weigh(nc.gpsimd, 1, "scratch0")
+        add(1)
+        subtract(2, "scratch0")
+        weigh(nc.gpsimd, 2, "scratch1")
         add(2)
-        subtract(3)
-        weigh(nc.gpsimd, 3)
+        subtract(3, "scratch1")
+        weigh(nc.gpsimd, 3, "scratch0")
         for t in range(PACK):
-            put(t)
+            scatter_and_store(t)
 
         y_codes = keep.tile([P, U], U32, name="y_codes", align_bytes=64)
         y_scales = keep.tile([P, U], U8, name="y_scales", align_bytes=64)
         words = out_1.rearrange("z l c r -> (z l) (c r)").bitcast(I32)
-        last = PACK - 1
-        for c in range(len(SHARES)):
-            round_out(nc.scalar.copy if c else nc.vector.tensor_copy, last, *SHARES[c])
+        for c, (lo, hi) in enumerate(SHARES):
+            round_out(nc.scalar.copy if c else nc.vector.tensor_copy, LAST, lo, hi)
         for c in (1, 0, 2):
             cols = slice(*SHARES[c])
             nc.vector.quantize_mx(y_codes[:, cols].bitcast(FP8X4), y_scales[:, cols], y_bf[:, cols, :].rearrange("p c r -> p (c r)"))
             nc.sync.dma_start(words[:, cols], y_codes[:, cols].bitcast(I32))
         scale_rows = out_2.rearrange("z q c -> (z q) c").bitcast(I32)
-        for q in range(4):
+        for q in range(P // 32):
             queue = nc.scalar if q % 2 else nc.sync
             queue.dma_start(scale_rows[4 * q : 4 * q + 4, :], y_scales[32 * q : 32 * q + 4, :].bitcast(I32))

@@ -19,6 +19,7 @@ P = 128
 PACK = 4
 LAST = PACK - 1
 HALF = N // 2
+PIECES = {"w1": ((0, 256), (256, 512)), "w2": ((0, 256), (256, 384), (384, 512))}
 SHARES = ((0, 512), (512, 768), (768, 1024))
 
 
@@ -31,7 +32,7 @@ def tile_picked_gmem_tanh_lo_kernel(tc, xT, mem, w1, w2, offs, slot, out_0, out_
         offs_t = keep.tile([P, S // 16], U16, name="offs_t")
         slot_t = keep.tile([P, S // 16], U16, name="slot_t")
         x_raw = [keep.tile([P, T], F32, name=f"x_raw{j}") for j in range(PACK)]
-        w_raw = {(w, h): keep.tile([P, PACK, HALF], F32, name=f"{w}_raw{h}") for w in ("w1", "w2") for h in range(2)}
+        w_raw = {(w, lo): keep.tile([P, PACK, hi - lo], F32, name=f"{w}_raw{lo}") for w in PIECES for lo, hi in PIECES[w]}
         page = [keep.tile([P, U], F32, name=f"page{t}") for t in range(LAST)]
 
         x_rows = xT.rearrange("(p j) c -> p j c", j=PACK)
@@ -44,8 +45,8 @@ def tile_picked_gmem_tanh_lo_kernel(tc, xT, mem, w1, w2, offs, slot, out_0, out_
                 nc.sync.dma_start(offs_t[:], offs)
         for which, w in (("w1", w1), ("w2", w2)):
             w_rows = w.rearrange("(p j) c -> p j c", j=PACK)
-            for h in range(2):
-                nc.sync.dma_start(w_raw[which, h][:], w_rows[:, :, h * HALF : (h + 1) * HALF])
+            for lo, hi in PIECES[which]:
+                nc.sync.dma_start(w_raw[which, lo][:], w_rows[:, :, lo:hi])
         nc.sync.dma_start(slot_t[:], slot)
         for t in range(LAST):
             nc.sync.dma_start(page[t][:], mem_rows[:, t, :])
@@ -71,23 +72,34 @@ def tile_picked_gmem_tanh_lo_kernel(tc, xT, mem, w1, w2, offs, slot, out_0, out_
         x_scales = keep.tile([P, S], U8, name="x_scales", align_bytes=64)
         nc.vector.quantize_mx(x_codes[:].bitcast(FP8X4), x_scales[:], x_bf[:].rearrange("p c j -> p (c j)"))
 
-        w_bf = {w: keep.tile([P, PACK, P, PACK], BF16, name=f"{w}_bf", tag=f"{w}_bf", align_bytes=64) for w in ("w1", "w2")}
+        w1_bf = keep.tile([P, PACK, P, PACK], BF16, name="w1_bf", tag="w1_bf", align_bytes=64)
+        w2_bf = [keep.tile([P, PACK, P // 2, PACK], BF16, name=f"w2_bf{h}", tag=f"w2_bf{h}", align_bytes=64) for h in range(2)]
 
-        def regroup_w(copy, which, h):
-            dst = w_bf[which][:].rearrange("p t m j -> p m j t")
-            src = w_raw[which, h][:].rearrange("p j (m t) -> p m j t", t=PACK)
-            copy(dst[:, h * (P // 2) : (h + 1) * (P // 2)], src)
+        def regroup_w(copy, which, piece, dst, first):
+            lo, hi = PIECES[which][piece]
+            src = w_raw[which, lo][:].rearrange("p j (m t) -> p m j t", t=PACK)
+            copy(dst[:].rearrange("p t m j -> p m j t")[:, (lo - first) // PACK : (hi - first) // PACK], src)
 
         stationary = {}
 
-        def quantize_w(which, t0, t1):
+        def code_tiles(which, t0, t1):
             width = (t1 - t0) * P
             codes = keep.tile([P, width], U32, name=f"{which}_codes{t0}", align_bytes=64)
             scales = keep.tile([P, width], U8, name=f"{which}_scales{t0}", align_bytes=64)
-            nc.vector.quantize_mx(codes[:].bitcast(FP8X4), scales[:], w_bf[which][:, t0:t1, :, :].rearrange("p t m j -> p (t m j)"))
             for t in range(t0, t1):
                 cols = slice((t - t0) * P, (t - t0 + 1) * P)
                 stationary[which, t] = (codes[:, cols], scales[:, cols])
+            return codes, scales
+
+        def quantize_w1(t0, t1):
+            codes, scales = code_tiles("w1", t0, t1)
+            nc.vector.quantize_mx(codes[:].bitcast(FP8X4), scales[:], w1_bf[:, t0:t1, :, :].rearrange("p t m j -> p (t m j)"))
+
+        def quantize_w2(h):
+            cols = slice(h * P // 2, (h + 1) * P // 2)
+            for t in range(PACK):
+                codes, scales = stationary["w2", t]
+                nc.vector.quantize_mx(codes[:, cols].bitcast(FP8X4), scales[:, cols], w2_bf[h][:, t, :, :].rearrange("p m j -> p (m j)"))
 
         def product(which, t, bank):
             acc = psum.tile([P, S], F32, name=f"{which}_acc{t}", tag=bank)
@@ -151,17 +163,20 @@ def tile_picked_gmem_tanh_lo_kernel(tc, xT, mem, w1, w2, offs, slot, out_0, out_
                 nc.scalar.copy(y_bf[:, lo:hi, 2:4], page[t][:, lo:hi].unsqueeze(2).to_broadcast([P, hi - lo, 2]))
                 round_out(nc.scalar.copy, t, hi, U)
 
-        regroup_w(nc.scalar.copy, "w1", 0)
-        regroup_w(nc.scalar.copy, "w1", 1)
-        quantize_w("w1", 0, 1)
-        quantize_w("w1", 1, 2)
-        quantize_w("w1", 2, PACK)
-        regroup_w(nc.scalar.copy, "w2", 0)
-        regroup_w(nc.vector.tensor_copy, "w2", 1)
+        regroup_w(nc.scalar.copy, "w1", 0, w1_bf, 0)
+        regroup_w(nc.scalar.copy, "w1", 1, w1_bf, 0)
+        quantize_w1(0, 1)
+        quantize_w1(1, 2)
+        quantize_w1(2, PACK)
+        regroup_w(nc.scalar.copy, "w2", 0, w2_bf[0], 0)
+        regroup_w(nc.vector.tensor_copy, "w2", 1, w2_bf[1], HALF)
+        regroup_w(nc.vector.tensor_copy, "w2", 2, w2_bf[1], HALF)
         candidate(0, "bank0")
-        quantize_w("w2", 0, PACK)
+        code_tiles("w2", 0, PACK)
+        quantize_w2(0)
+        quantize_w2(1)
 
-        page.append(keep.tile([P, U], F32, name=f"page{LAST}", tag="w2_bf", align_bytes=64))
+        page.append(keep.tile([P, U], F32, name=f"page{LAST}", tag="w2_bf1", align_bytes=64))
         nc.scalar.dma_start(page[LAST][:], mem_rows[:, LAST, :])
 
         candidate(1, "bank1")

@@ -19,7 +19,7 @@ P = 128
 PACK = 4
 LAST = PACK - 1
 HALF = N // 2
-PIECES = {"w1": ((0, 256), (256, 512)), "w2": ((0, 256), (256, 384), (384, 512))}
+PIECES = {"w1": ((0, 256), (256, 512)), "w2": ((0, 256), (256, 512))}
 SHARES = ((0, 512), (512, 768), (768, 1024))
 
 
@@ -170,7 +170,6 @@ def tile_picked_gmem_tanh_lo_kernel(tc, xT, mem, w1, w2, offs, slot, out_0, out_
         quantize_w1(2, PACK)
         regroup_w(nc.scalar.copy, "w2", 0, w2_bf[0], 0)
         regroup_w(nc.vector.tensor_copy, "w2", 1, w2_bf[1], HALF)
-        regroup_w(nc.vector.tensor_copy, "w2", 2, w2_bf[1], HALF)
         candidate(0, "bank0")
         code_tiles("w2", 0, PACK)
         quantize_w2(0)

@@ -101,15 +101,15 @@ def tile_picked_gmem_tanh_lo_kernel(tc, xT, mem, w1, w2, offs, slot, out_0, out_
                 codes, scales = stationary["w2", t]
                 nc.vector.quantize_mx(codes[:, cols].bitcast(FP8X4), scales[:, cols], w2_bf[h][:, t, :, :].rearrange("p m j -> p (m j)"))
 
-        def product(which, t, bank):
-            acc = psum.tile([P, S], F32, name=f"{which}_acc{t}", tag=bank)
+        def product(which, t, bank, lo=0, hi=S):
+            acc = psum.tile([P, hi - lo], F32, name=f"{which}_acc{t}_{lo}", tag=bank)
             codes, scales = stationary[which, t]
             nc.tensor.matmul_mx(
                 acc[:],
                 lhsT=codes.bitcast(FP8X4),
                 lhsT_scale=scales,
-                rhs=x_codes[:].bitcast(FP8X4),
-                rhs_scale=x_scales[:],
+                rhs=x_codes[:, lo:hi].bitcast(FP8X4),
+                rhs_scale=x_scales[:, lo:hi],
                 start=True,
                 stop=True,
             )
@@ -124,8 +124,8 @@ def tile_picked_gmem_tanh_lo_kernel(tc, xT, mem, w1, w2, offs, slot, out_0, out_
         old = {t: keep.tile([P, S], F32, name=f"old{t}") for t in range(2, PACK)}
         y_bf = keep.tile([P, U, PACK], BF16, name="y_bf", align_bytes=64)
 
-        def candidate(t, bank):
-            nc.scalar.activation(cand[:, t, :], product("w1", t, bank)[:], ACT.Tanh)
+        def candidate(t, bank, lo=0, hi=S):
+            nc.scalar.activation(cand[:, t, lo:hi], product("w1", t, bank, lo, hi)[:], ACT.Tanh)
 
         def gate(t, bank):
             nc.scalar.activation(stay[:, t, :], product("w2", t, bank)[:], ACT.Sigmoid, scale=-1.0)
@@ -170,7 +170,8 @@ def tile_picked_gmem_tanh_lo_kernel(tc, xT, mem, w1, w2, offs, slot, out_0, out_
         quantize_w1(2, PACK)
         regroup_w(nc.scalar.copy, "w2", 0, w2_bf[0], 0)
         regroup_w(nc.vector.tensor_copy, "w2", 1, w2_bf[1], HALF)
-        candidate(0, "bank0")
+        candidate(0, "bank0", 0, S // 2)
+        candidate(0, "bank7", S // 2, S)
         code_tiles("w2", 0, PACK)
         quantize_w2(0)
         quantize_w2(1)

@@ -59,26 +59,29 @@ def tile_picked_gmem_tanh_lo_kernel(tc, xT, mem, w1, w2, offs, slot, out_0, out_
         picked = [keep.tile([P, 2, S], F32, name=f"picked{pair}") for pair in range(2)]
         x_bf = keep.tile([P, S, PACK], BF16, name="x_bf", align_bytes=64)
 
-        def interleave_x(copy, pair):
-            copy(x_bf[:, :, 2 * pair : 2 * pair + 2], picked[pair][:].rearrange("p e c -> p c e"))
+        def interleave_x(copy, pair, lo, hi):
+            copy(x_bf[:, lo:hi, 2 * pair : 2 * pair + 2], picked[pair][:, :, lo:hi].rearrange("p e c -> p c e"))
 
         for j in range(PACK):
             nc.vector.tensor_copy(picked[j // 2][:, j % 2, :], x_raw[j][:].indirect(offs_t[:]))
             if j == 1:
-                interleave_x(nc.scalar.copy, 0)
-        interleave_x(nc.vector.tensor_copy, 1)
+                interleave_x(nc.scalar.copy, 0, 0, S)
+        x_halves = ((0, S // 2), (S // 2, S))
+        for lo, hi in x_halves:
+            interleave_x(nc.vector.tensor_copy, 1, lo, hi)
 
         x_codes = keep.tile([P, S], U32, name="x_codes", align_bytes=64)
         x_scales = keep.tile([P, S], U8, name="x_scales", align_bytes=64)
-        nc.vector.quantize_mx(x_codes[:].bitcast(FP8X4), x_scales[:], x_bf[:].rearrange("p c j -> p (c j)"))
+        for lo, hi in x_halves:
+            nc.vector.quantize_mx(x_codes[:, lo:hi].bitcast(FP8X4), x_scales[:, lo:hi], x_bf[:, lo:hi, :].rearrange("p c j -> p (c j)"))
 
-        w1_bf = keep.tile([P, PACK, P, PACK], BF16, name="w1_bf", tag="w1_bf", align_bytes=64)
+        w1_bf = [keep.tile([P, 2, P, PACK], BF16, name=f"w1_bf{pair}", align_bytes=64) for pair in range(2)]
         w2_bf = [keep.tile([P, PACK, P // 2, PACK], BF16, name=f"w2_bf{h}", tag=f"w2_bf{h}", align_bytes=64) for h in range(2)]
 
-        def regroup_w(copy, which, piece, dst, first):
+        def regroup_w(copy, which, piece, dst, first, t0=0, t1=PACK):
             lo, hi = PIECES[which][piece]
             src = w_raw[which, lo][:].rearrange("p j (m t) -> p m j t", t=PACK)
-            copy(dst[:].rearrange("p t m j -> p m j t")[:, (lo - first) // PACK : (hi - first) // PACK], src)
+            copy(dst[:].rearrange("p t m j -> p m j t")[:, (lo - first) // PACK : (hi - first) // PACK], src[:, :, :, t0:t1])
 
         stationary = {}
 
@@ -93,7 +96,7 @@ def tile_picked_gmem_tanh_lo_kernel(tc, xT, mem, w1, w2, offs, slot, out_0, out_
 
         def quantize_w1(t0, t1):
             codes, scales = code_tiles("w1", t0, t1)
-            nc.vector.quantize_mx(codes[:].bitcast(FP8X4), scales[:], w1_bf[:, t0:t1, :, :].rearrange("p t m j -> p (t m j)"))
+            nc.vector.quantize_mx(codes[:].bitcast(FP8X4), scales[:], w1_bf[t0 // 2][:, t0 % 2 : t0 % 2 + t1 - t0, :, :].rearrange("p t m j -> p (t m j)"))
 
         def quantize_w2(h):
             cols = slice(h * P // 2, (h + 1) * P // 2)
@@ -163,8 +166,9 @@ def tile_picked_gmem_tanh_lo_kernel(tc, xT, mem, w1, w2, offs, slot, out_0, out_
                 nc.scalar.copy(y_bf[:, lo:hi, 2:4], page[t][:, lo:hi].unsqueeze(2).to_broadcast([P, hi - lo, 2]))
                 round_out(nc.scalar.copy, t, hi, U)
 
-        regroup_w(nc.scalar.copy, "w1", 0, w1_bf, 0)
-        regroup_w(nc.scalar.copy, "w1", 1, w1_bf, 0)
+        for piece in range(2):
+            for pair in range(2):
+                regroup_w(nc.scalar.copy, "w1", piece, w1_bf[pair], 0, 2 * pair, 2 * pair + 2)
         quantize_w1(0, 1)
         quantize_w1(1, 2)
         quantize_w1(2, PACK)

@@ -20,7 +20,8 @@ PACK = 4
 LAST = PACK - 1
 HALF = N // 2
 PIECES = {"w1": ((0, 256), (256, 512)), "w2": ((0, 256), (256, 512))}
-SHARES = ((0, 512), (512, 768), (768, 1024))
+SHARES = ((0, 384), (384, 640), (640, 1024))
+LIST_HALVES = ((0, S // 2), (S // 2, S))
 
 
 def tile_picked_gmem_tanh_lo_kernel(tc, xT, mem, w1, w2, offs, slot, out_0, out_1, out_2):
@@ -33,7 +34,7 @@ def tile_picked_gmem_tanh_lo_kernel(tc, xT, mem, w1, w2, offs, slot, out_0, out_
         slot_t = keep.tile([P, S // 16], U16, name="slot_t")
         x_raw = [keep.tile([P, T], F32, name=f"x_raw{j}") for j in range(PACK)]
         w_raw = {(w, lo): keep.tile([P, PACK, hi - lo], F32, name=f"{w}_raw{lo}") for w in PIECES for lo, hi in PIECES[w]}
-        page = [keep.tile([P, U], F32, name=f"page{t}") for t in range(LAST)]
+        page = [keep.tile([P, U], F32, name=f"page{t}") for t in range(PACK)]
 
         x_rows = xT.rearrange("(p j) c -> p j c", j=PACK)
         mem_rows = mem.rearrange("(p t) c -> p t c", t=PACK)
@@ -48,12 +49,12 @@ def tile_picked_gmem_tanh_lo_kernel(tc, xT, mem, w1, w2, offs, slot, out_0, out_
             for lo, hi in PIECES[which]:
                 nc.sync.dma_start(w_raw[which, lo][:], w_rows[:, :, lo:hi])
         nc.sync.dma_start(slot_t[:], slot)
-        for t in range(LAST):
+        for t in range(PACK):
             nc.sync.dma_start(page[t][:], mem_rows[:, t, :])
 
         warm_in = keep.tile([P, 1], F32, name="warm_in")
         warm_out = keep.tile([P, 1], F32, name="warm_out")
-        nc.gpsimd.memset(warm_in[:], 0.0)
+        nc.vector.memset(warm_in[:], 0.0)
         nc.scalar.activation(warm_out[:], warm_in[:], ACT.Sigmoid)
 
         picked = [keep.tile([P, 2, S], F32, name=f"picked{pair}") for pair in range(2)]
@@ -118,53 +119,20 @@ def tile_picked_gmem_tanh_lo_kernel(tc, xT, mem, w1, w2, offs, slot, out_0, out_
             )
             return acc
 
-        cand = keep.tile([P, PACK, S], F32, name="cand")
+        cand = [keep.tile([P, S], F32, name=f"cand{t}", tag=f"cand{t}", align_bytes=64) for t in range(PACK)]
         stay = keep.tile([P, PACK, S], F32, name="stay")
-        diff_fused = keep.tile([P, 2, S], F32, name="diff_fused")
-        diff = {t: diff_fused[:, t, :] for t in range(2)}
-        kept = {}
+        diff = keep.tile([P, PACK, S], F32, name="diff")
+        kept = [keep.tile([P, S], F32, name=f"kept{t}", tag=f"kept{t}", align_bytes=64) for t in range(PACK)]
         new = keep.tile([P, LAST, S], F32, name="new")
-        old = {t: keep.tile([P, S], F32, name=f"old{t}") for t in range(2, PACK)}
-        y_bf = keep.tile([P, U, PACK], BF16, name="y_bf", align_bytes=64)
 
         def candidate(t, bank, lo=0, hi=S):
-            nc.scalar.activation(cand[:, t, lo:hi], product("w1", t, bank, lo, hi)[:], ACT.Tanh)
+            nc.scalar.activation(cand[t][:, lo:hi], product("w1", t, bank, lo, hi)[:], ACT.Tanh)
 
         def gate(t, bank):
             nc.scalar.activation(stay[:, t, :], product("w2", t, bank)[:], ACT.Sigmoid, scale=-1.0)
 
-        def gather_and_subtract(t):
-            nc.vector.tensor_tensor(diff[t], page[t][:].indirect(slot_t[:]), cand[:, t, :], ALU.subtract)
-
-        def gather(t):
-            nc.vector.tensor_copy(old[t][:], page[t][:].indirect(slot_t[:]))
-
-        def subtract(t, scratch):
-            diff[t] = keep.tile([P, S], F32, name=f"diff{t}", tag=scratch)[:]
-            nc.gpsimd.tensor_tensor(diff[t], old[t][:], cand[:, t, :], ALU.subtract)
-
-        def weigh(engine, t, scratch):
-            kept[t] = keep.tile([P, S], F32, name=f"kept{t}", tag=scratch)[:]
-            engine.tensor_tensor(kept[t], diff[t], stay[:, t, :], ALU.mult)
-
-        def add(t):
-            nc.gpsimd.tensor_tensor(new[:, t, :], kept[t], cand[:, t, :], ALU.add)
-
-        def round_out(copy, t, lo, hi):
-            copy(y_bf[:, lo:hi, t], page[t][:, lo:hi])
-
-        def scatter_and_store(t):
-            if t < LAST:
-                nc.vector.tensor_copy(page[t][:].indirect(slot_t[:]), new[:, t, :])
-            else:
-                nc.vector.tensor_tensor(page[t][:].indirect(slot_t[:]), kept[t], cand[:, t, :], ALU.add)
-            nc.sync.dma_start(out_rows[:, t, :], page[t][:])
-            if t < LAST - 1:
-                round_out(nc.scalar.copy, t, 0, U)
-            elif t == LAST - 1:
-                lo, hi = SHARES[0]
-                nc.scalar.copy(y_bf[:, lo:hi, 2:4], page[t][:, lo:hi].unsqueeze(2).to_broadcast([P, hi - lo, 2]))
-                round_out(nc.scalar.copy, t, hi, U)
+        def entries(lo, hi):
+            return slot_t[:, lo // 16 : hi // 16]
 
         for piece in range(2):
             for pair in range(2):
@@ -179,10 +147,6 @@ def tile_picked_gmem_tanh_lo_kernel(tc, xT, mem, w1, w2, offs, slot, out_0, out_
         code_tiles("w2", 0, PACK)
         quantize_w2(0)
         quantize_w2(1)
-
-        page.append(keep.tile([P, U], F32, name=f"page{LAST}", tag="w2_bf1", align_bytes=64))
-        nc.scalar.dma_start(page[LAST][:], mem_rows[:, LAST, :])
-
         candidate(1, "bank1")
         candidate(2, "bank2")
         gate(0, "bank1")
@@ -191,31 +155,37 @@ def tile_picked_gmem_tanh_lo_kernel(tc, xT, mem, w1, w2, offs, slot, out_0, out_
         gate(2, "bank5")
         gate(3, "bank6")
 
-        gather_and_subtract(0)
-        gather_and_subtract(1)
-        weigh(nc.vector, 0, "scratch0")
-        add(0)
-        gather(2)
-        gather(3)
-        weigh(nc.gpsimd, 1, "scratch0")
-        add(1)
-        subtract(2, "scratch0")
-        weigh(nc.gpsimd, 2, "scratch1")
-        add(2)
-        subtract(3, "scratch1")
-        weigh(nc.gpsimd, 3, "scratch0")
         for t in range(PACK):
-            scatter_and_store(t)
+            for lo, hi in LIST_HALVES:
+                nc.vector.tensor_tensor(diff[:, t, lo:hi], page[t][:].indirect(entries(lo, hi)), cand[t][:, lo:hi], ALU.subtract)
+            for lo, hi in LIST_HALVES:
+                nc.vector.tensor_tensor(kept[t][:, lo:hi], diff[:, t, lo:hi], stay[:, t, lo:hi], ALU.mult)
+            if t < LAST:
+                for lo, hi in LIST_HALVES:
+                    nc.vector.tensor_tensor(new[:, t, lo:hi], kept[t][:, lo:hi], cand[t][:, lo:hi], ALU.add)
+                for lo, hi in LIST_HALVES:
+                    nc.scalar.activation(page[t][:].indirect(entries(lo, hi)), new[:, t, lo:hi], ACT.Copy)
+            else:
+                nc.vector.tensor_tensor(page[t][:].indirect(slot_t[:]), kept[t][:], cand[t][:], ALU.add)
+            nc.sync.dma_start(out_rows[:, t, :], page[t][:])
 
         y_codes = keep.tile([P, U], U32, name="y_codes", align_bytes=64)
         y_scales = keep.tile([P, U], U8, name="y_scales", align_bytes=64)
         words = out_1.rearrange("z l c r -> (z l) (c r)").bitcast(I32)
+        y_bf = {}
         for c, (lo, hi) in enumerate(SHARES):
-            round_out(nc.scalar.copy if c else nc.vector.tensor_copy, LAST, lo, hi)
-        for c in (1, 0, 2):
-            cols = slice(*SHARES[c])
-            nc.vector.quantize_mx(y_codes[:, cols].bitcast(FP8X4), y_scales[:, cols], y_bf[:, cols, :].rearrange("p c r -> p (c r)"))
-            nc.sync.dma_start(words[:, cols], y_codes[:, cols].bitcast(I32))
+            copy, word = (nc.scalar.copy, U32) if c == 2 else (nc.vector.tensor_copy, I32)
+            couples = keep.tile([P, 2, hi - lo, 2], BF16, name=f"couples{c}", tag=(f"kept{LAST}", f"cand{LAST}", "couples")[c], align_bytes=64)
+            y_bf[c] = keep.tile([P, (hi - lo) * PACK], BF16, name=f"y_bf{c}", align_bytes=64)
+            for t in (0, 1, 3, 2) if c < 2 else range(PACK):
+                copy(couples[:, t // 2, :, t % 2], page[t][:, lo:hi])
+            copy(
+                y_bf[c][:].bitcast(word).rearrange("p (c h) -> p c h", h=2),
+                couples[:].rearrange("p h c i -> p h (c i)").bitcast(word).rearrange("p h c -> p c h"),
+            )
+        for c, (lo, hi) in enumerate(SHARES):
+            nc.vector.quantize_mx(y_codes[:, lo:hi].bitcast(FP8X4), y_scales[:, lo:hi], y_bf[c][:])
+            nc.sync.dma_start(words[:, lo:hi], y_codes[:, lo:hi].bitcast(I32))
         scale_rows = out_2.rearrange("z q c -> (z q) c").bitcast(I32)
         for q in range(P // 32):
             queue = nc.scalar if q % 2 else nc.sync

@@ -18,10 +18,9 @@ ACT = mybir.ActivationFunctionType
 P = 128
 PACK = 4
 LAST = PACK - 1
-HALF = N // 2
-PIECES = {"w1": ((0, 256), (256, 512)), "w2": ((0, 256), (256, 512))}
-SHARES = ((0, 384), (384, 640), (640, 1024))
+W_HALVES = ((0, N // 2), (N // 2, N))
 LIST_HALVES = ((0, S // 2), (S // 2, S))
+SHARES = ((0, 256, "scalar"), (256, 768, "vector"), (768, 1024, "scalar"))
 
 
 def tile_picked_gmem_tanh_lo_kernel(tc, xT, mem, w1, w2, offs, slot, out_0, out_1, out_2):
@@ -33,7 +32,7 @@ def tile_picked_gmem_tanh_lo_kernel(tc, xT, mem, w1, w2, offs, slot, out_0, out_
         offs_t = keep.tile([P, S // 16], U16, name="offs_t")
         slot_t = keep.tile([P, S // 16], U16, name="slot_t")
         x_raw = [keep.tile([P, T], F32, name=f"x_raw{j}") for j in range(PACK)]
-        w_raw = {(w, lo): keep.tile([P, PACK, hi - lo], F32, name=f"{w}_raw{lo}") for w in PIECES for lo, hi in PIECES[w]}
+        w_raw = {(w, h): keep.tile([P, PACK, N // 2], F32, name=f"{w}_raw{h}") for w in ("w1", "w2") for h in range(2)}
         page = [keep.tile([P, U], F32, name=f"page{t}") for t in range(PACK)]
 
         x_rows = xT.rearrange("(p j) c -> p j c", j=PACK)
@@ -46,8 +45,8 @@ def tile_picked_gmem_tanh_lo_kernel(tc, xT, mem, w1, w2, offs, slot, out_0, out_
                 nc.sync.dma_start(offs_t[:], offs)
         for which, w in (("w1", w1), ("w2", w2)):
             w_rows = w.rearrange("(p j) c -> p j c", j=PACK)
-            for lo, hi in PIECES[which]:
-                nc.sync.dma_start(w_raw[which, lo][:], w_rows[:, :, lo:hi])
+            for h, (lo, hi) in enumerate(W_HALVES):
+                nc.sync.dma_start(w_raw[which, h][:], w_rows[:, :, lo:hi])
         nc.sync.dma_start(slot_t[:], slot)
         for t in range(PACK):
             nc.sync.dma_start(page[t][:], mem_rows[:, t, :])
@@ -57,53 +56,53 @@ def tile_picked_gmem_tanh_lo_kernel(tc, xT, mem, w1, w2, offs, slot, out_0, out_
         nc.vector.memset(warm_in[:], 0.0)
         nc.scalar.activation(warm_out[:], warm_in[:], ACT.Sigmoid)
 
+        def entries(offsets, lo, hi):
+            return offsets[:, lo // 16 : hi // 16]
+
         picked = [keep.tile([P, 2, S], F32, name=f"picked{pair}") for pair in range(2)]
         x_bf = keep.tile([P, S, PACK], BF16, name="x_bf", align_bytes=64)
 
         def interleave_x(copy, pair, lo, hi):
             copy(x_bf[:, lo:hi, 2 * pair : 2 * pair + 2], picked[pair][:, :, lo:hi].rearrange("p e c -> p c e"))
 
-        for j in range(PACK):
-            nc.vector.tensor_copy(picked[j // 2][:, j % 2, :], x_raw[j][:].indirect(offs_t[:]))
-            if j == 1:
-                interleave_x(nc.scalar.copy, 0, 0, S)
-        x_halves = ((0, S // 2), (S // 2, S))
-        for lo, hi in x_halves:
-            interleave_x(nc.vector.tensor_copy, 1, lo, hi)
+        def gather_x(engine, j, lo, hi):
+            dst, src = picked[j // 2][:, j % 2, lo:hi], x_raw[j][:].indirect(entries(offs_t, lo, hi))
+            if engine == "vector":
+                nc.vector.tensor_copy(dst, src)
+            else:
+                nc.scalar.activation(dst, src, ACT.Copy)
 
-        x_codes = keep.tile([P, S], U32, name="x_codes", align_bytes=64)
-        x_scales = keep.tile([P, S], U8, name="x_scales", align_bytes=64)
-        for lo, hi in x_halves:
-            nc.vector.quantize_mx(x_codes[:, lo:hi].bitcast(FP8X4), x_scales[:, lo:hi], x_bf[:, lo:hi, :].rearrange("p c j -> p (c j)"))
+        first, second = LIST_HALVES
+        gather_x("vector", 0, 0, S)
+        gather_x("scalar", 1, 0, S)
+        gather_x("scalar", 2, 0, S)
+        interleave_x(nc.vector.tensor_copy, 0, 0, S)
+        gather_x("vector", LAST, *first)
+        gather_x("scalar", LAST, *second)
+        interleave_x(nc.vector.tensor_copy, 1, *first)
+        interleave_x(nc.scalar.copy, 1, *second)
 
-        w1_bf = [keep.tile([P, 2, P, PACK], BF16, name=f"w1_bf{pair}", align_bytes=64) for pair in range(2)]
-        w2_bf = [keep.tile([P, PACK, P // 2, PACK], BF16, name=f"w2_bf{h}", tag=f"w2_bf{h}", align_bytes=64) for h in range(2)]
+        w_bf = {(w, pair): keep.tile([P, 2, P, PACK], BF16, name=f"{w}_bf{pair}", align_bytes=64) for w in ("w1", "w2") for pair in range(2)}
 
-        def regroup_w(copy, which, piece, dst, first, t0=0, t1=PACK):
-            lo, hi = PIECES[which][piece]
-            src = w_raw[which, lo][:].rearrange("p j (m t) -> p m j t", t=PACK)
-            copy(dst[:].rearrange("p t m j -> p m j t")[:, (lo - first) // PACK : (hi - first) // PACK], src[:, :, :, t0:t1])
+        def regroup_w(copy, which, h, pair):
+            src = w_raw[which, h][:].rearrange("p j (m t) -> p m j t", t=PACK)
+            dst = w_bf[which, pair][:].rearrange("p i m j -> p m j i")
+            copy(dst[:, h * P // 2 : (h + 1) * P // 2], src[:, :, :, 2 * pair : 2 * pair + 2])
 
         stationary = {}
 
-        def code_tiles(which, t0, t1):
+        def quantize_w(which, t0, t1):
             width = (t1 - t0) * P
             codes = keep.tile([P, width], U32, name=f"{which}_codes{t0}", align_bytes=64)
             scales = keep.tile([P, width], U8, name=f"{which}_scales{t0}", align_bytes=64)
             for t in range(t0, t1):
                 cols = slice((t - t0) * P, (t - t0 + 1) * P)
                 stationary[which, t] = (codes[:, cols], scales[:, cols])
-            return codes, scales
+            values = w_bf[which, t0 // 2][:, t0 % 2 : t0 % 2 + t1 - t0, :, :]
+            nc.vector.quantize_mx(codes[:].bitcast(FP8X4), scales[:], values.rearrange("p t m j -> p (t m j)"))
 
-        def quantize_w1(t0, t1):
-            codes, scales = code_tiles("w1", t0, t1)
-            nc.vector.quantize_mx(codes[:].bitcast(FP8X4), scales[:], w1_bf[t0 // 2][:, t0 % 2 : t0 % 2 + t1 - t0, :, :].rearrange("p t m j -> p (t m j)"))
-
-        def quantize_w2(h):
-            cols = slice(h * P // 2, (h + 1) * P // 2)
-            for t in range(PACK):
-                codes, scales = stationary["w2", t]
-                nc.vector.quantize_mx(codes[:, cols].bitcast(FP8X4), scales[:, cols], w2_bf[h][:, t, :, :].rearrange("p m j -> p (m j)"))
+        x_codes = keep.tile([P, S], U32, name="x_codes", align_bytes=64)
+        x_scales = keep.tile([P, S], U8, name="x_scales", align_bytes=64)
 
         def product(which, t, bank, lo=0, hi=S):
             acc = psum.tile([P, hi - lo], F32, name=f"{which}_acc{t}_{lo}", tag=bank)
@@ -119,72 +118,67 @@ def tile_picked_gmem_tanh_lo_kernel(tc, xT, mem, w1, w2, offs, slot, out_0, out_
             )
             return acc
 
-        cand = [keep.tile([P, S], F32, name=f"cand{t}", tag=f"cand{t}", align_bytes=64) for t in range(PACK)]
-        stay = keep.tile([P, PACK, S], F32, name="stay")
-        diff = keep.tile([P, PACK, S], F32, name="diff")
+        regroup_w(nc.vector.tensor_copy, "w1", 0, 0)
+        for lo, hi in LIST_HALVES:
+            nc.vector.quantize_mx(x_codes[:, lo:hi].bitcast(FP8X4), x_scales[:, lo:hi], x_bf[:, lo:hi, :].rearrange("p c j -> p (c j)"))
+        regroup_w(nc.vector.tensor_copy, "w1", 1, 0)
+        for h in range(2):
+            regroup_w(nc.scalar.copy, "w1", h, 1)
+        quantize_w("w1", 0, 1)
+        quantize_w("w1", 1, 2)
+        quantize_w("w1", 2, PACK)
+        for h in range(2):
+            for pair in range(2):
+                regroup_w(nc.vector.tensor_copy, "w2", h, pair)
+        quantize_w("w2", 0, 1)
+        quantize_w("w2", 1, 2)
+        quantize_w("w2", 2, PACK)
+
+        cand = keep.tile([P, PACK, S], F32, name="cand")
+        stay = [keep.tile([P, S], F32, name=f"stay{t}", tag=f"stay{t}", align_bytes=64) for t in range(PACK)]
+        diff = [keep.tile([P, S], F32, name=f"diff{t}", tag=f"diff{t}", align_bytes=64) for t in range(PACK)]
         kept = [keep.tile([P, S], F32, name=f"kept{t}", tag=f"kept{t}", align_bytes=64) for t in range(PACK)]
         new = keep.tile([P, LAST, S], F32, name="new")
 
-        def candidate(t, bank, lo=0, hi=S):
-            nc.scalar.activation(cand[t][:, lo:hi], product("w1", t, bank, lo, hi)[:], ACT.Tanh)
+        for lo, hi in LIST_HALVES:
+            nc.scalar.activation(cand[:, 0, lo:hi], product("w1", 0, f"bank{lo}", lo, hi)[:], ACT.Tanh)
+        for t in range(1, PACK):
+            nc.scalar.activation(cand[:, t, :], product("w1", t, f"bank{t}")[:], ACT.Tanh)
+        for t in range(PACK):
+            nc.scalar.activation(stay[t][:], product("w2", t, f"bank{PACK + t}" if t else "bank0")[:], ACT.Sigmoid, scale=-1.0)
 
-        def gate(t, bank):
-            nc.scalar.activation(stay[:, t, :], product("w2", t, bank)[:], ACT.Sigmoid, scale=-1.0)
-
-        def entries(lo, hi):
-            return slot_t[:, lo // 16 : hi // 16]
-
-        for piece in range(2):
-            for pair in range(2):
-                regroup_w(nc.scalar.copy, "w1", piece, w1_bf[pair], 0, 2 * pair, 2 * pair + 2)
-        quantize_w1(0, 1)
-        quantize_w1(1, 2)
-        quantize_w1(2, PACK)
-        regroup_w(nc.scalar.copy, "w2", 0, w2_bf[0], 0)
-        regroup_w(nc.vector.tensor_copy, "w2", 1, w2_bf[1], HALF)
-        candidate(0, "bank0", 0, S // 2)
-        candidate(0, "bank7", S // 2, S)
-        code_tiles("w2", 0, PACK)
-        quantize_w2(0)
-        quantize_w2(1)
-        candidate(1, "bank1")
-        candidate(2, "bank2")
-        gate(0, "bank1")
-        candidate(3, "bank3")
-        gate(1, "bank4")
-        gate(2, "bank5")
-        gate(3, "bank6")
+        rows = [keep.tile([P, PACK, hi - lo], F32, name=f"rows{lo}") for lo, hi, engine in SHARES]
 
         for t in range(PACK):
             for lo, hi in LIST_HALVES:
-                nc.vector.tensor_tensor(diff[:, t, lo:hi], page[t][:].indirect(entries(lo, hi)), cand[t][:, lo:hi], ALU.subtract)
+                nc.vector.tensor_tensor(diff[t][:, lo:hi], page[t][:].indirect(entries(slot_t, lo, hi)), cand[:, t, lo:hi], ALU.subtract)
             for lo, hi in LIST_HALVES:
-                nc.vector.tensor_tensor(kept[t][:, lo:hi], diff[:, t, lo:hi], stay[:, t, lo:hi], ALU.mult)
+                nc.vector.tensor_tensor(kept[t][:, lo:hi], diff[t][:, lo:hi], stay[t][:, lo:hi], ALU.mult)
             if t < LAST:
                 for lo, hi in LIST_HALVES:
-                    nc.vector.tensor_tensor(new[:, t, lo:hi], kept[t][:, lo:hi], cand[t][:, lo:hi], ALU.add)
+                    nc.vector.tensor_tensor(new[:, t, lo:hi], kept[t][:, lo:hi], cand[:, t, lo:hi], ALU.add)
                 for lo, hi in LIST_HALVES:
-                    nc.scalar.activation(page[t][:].indirect(entries(lo, hi)), new[:, t, lo:hi], ACT.Copy)
+                    nc.scalar.activation(page[t][:].indirect(entries(slot_t, lo, hi)), new[:, t, lo:hi], ACT.Copy)
             else:
-                nc.vector.tensor_tensor(page[t][:].indirect(slot_t[:]), kept[t][:], cand[t][:], ALU.add)
+                nc.vector.tensor_tensor(page[t][:].indirect(slot_t[:]), kept[t][:], cand[:, t, :], ALU.add)
+            if t < 2:
+                for c, (lo, hi, engine) in enumerate(SHARES):
+                    nc.sync.dma_start(rows[c][:, t, :], page[t][:, lo:hi])
             nc.sync.dma_start(out_rows[:, t, :], page[t][:])
 
         y_codes = keep.tile([P, U], U32, name="y_codes", align_bytes=64)
         y_scales = keep.tile([P, U], U8, name="y_scales", align_bytes=64)
         words = out_1.rearrange("z l c r -> (z l) (c r)").bitcast(I32)
-        y_bf = {}
-        for c, (lo, hi) in enumerate(SHARES):
-            copy, word = (nc.scalar.copy, U32) if c == 2 else (nc.vector.tensor_copy, I32)
-            couples = keep.tile([P, 2, hi - lo, 2], BF16, name=f"couples{c}", tag=(f"kept{LAST}", f"cand{LAST}", "couples")[c], align_bytes=64)
-            y_bf[c] = keep.tile([P, (hi - lo) * PACK], BF16, name=f"y_bf{c}", align_bytes=64)
-            for t in (0, 1, 3, 2) if c < 2 else range(PACK):
-                copy(couples[:, t // 2, :, t % 2], page[t][:, lo:hi])
-            copy(
-                y_bf[c][:].bitcast(word).rearrange("p (c h) -> p c h", h=2),
-                couples[:].rearrange("p h c i -> p h (c i)").bitcast(word).rearrange("p h c -> p c h"),
-            )
-        for c, (lo, hi) in enumerate(SHARES):
-            nc.vector.quantize_mx(y_codes[:, lo:hi].bitcast(FP8X4), y_scales[:, lo:hi], y_bf[c][:])
+        y_bf = [keep.tile([P, hi - lo, PACK], BF16, name=f"y_bf{lo}", align_bytes=64) for lo, hi, engine in SHARES]
+        copies = {"scalar": nc.scalar.copy, "vector": nc.vector.tensor_copy}
+        for c in (1, 0, 2):
+            lo, hi, engine = SHARES[c]
+            nc.scalar.copy(rows[c][:, 2, :], page[2][:, lo:hi])
+            nc.vector.tensor_copy(rows[c][:, LAST, :], page[LAST][:, lo:hi])
+        for c, (lo, hi, engine) in enumerate(SHARES):
+            copies[engine](y_bf[c][:], rows[c][:].rearrange("p t c -> p c t"))
+        for c, (lo, hi, engine) in enumerate(SHARES):
+            nc.vector.quantize_mx(y_codes[:, lo:hi].bitcast(FP8X4), y_scales[:, lo:hi], y_bf[c][:].rearrange("p c t -> p (c t)"))
             nc.sync.dma_start(words[:, lo:hi], y_codes[:, lo:hi].bitcast(I32))
         scale_rows = out_2.rearrange("z q c -> (z q) c").bitcast(I32)
         for q in range(P // 32):

@@ -118,7 +118,7 @@ def tile_picked_gmem_tanh_lo_kernel(tc, xT, mem, w1, w2, offs, slot, out_0, out_
             )
             return acc
 
-        regroup_w(nc.vector.tensor_copy, "w1", 0, 0)
+        regroup_w(nc.scalar.copy, "w1", 0, 0)
         for lo, hi in LIST_HALVES:
             nc.vector.quantize_mx(x_codes[:, lo:hi].bitcast(FP8X4), x_scales[:, lo:hi], x_bf[:, lo:hi, :].rearrange("p c j -> p (c j)"))
         regroup_w(nc.vector.tensor_copy, "w1", 1, 0)
@@ -176,7 +176,7 @@ def tile_picked_gmem_tanh_lo_kernel(tc, xT, mem, w1, w2, offs, slot, out_0, out_
             nc.scalar.copy(rows[c][:, 2, :], page[2][:, lo:hi])
             nc.vector.tensor_copy(rows[c][:, LAST, :], page[LAST][:, lo:hi])
         for c, (lo, hi, engine) in enumerate(SHARES):
-            copies[engine](y_bf[c][:], rows[c][:].rearrange("p t c -> p c t"))
+            copies[engine](y_bf[c][:].rearrange("p (g i) t -> p g t i", i=4), rows[c][:].rearrange("p t (g i) -> p g t i", i=4))
         for c, (lo, hi, engine) in enumerate(SHARES):
             nc.vector.quantize_mx(y_codes[:, lo:hi].bitcast(FP8X4), y_scales[:, lo:hi], y_bf[c][:].rearrange("p c t -> p (c t)"))
             nc.sync.dma_start(words[:, lo:hi], y_codes[:, lo:hi].bitcast(I32))

@@ -20,7 +20,8 @@ PACK = 4
 LAST = PACK - 1
 W_HALVES = ((0, N // 2), (N // 2, N))
 LIST_HALVES = ((0, S // 2), (S // 2, S))
-SHARES = ((0, 256, "scalar"), (256, 768, "vector"), (768, 1024, "scalar"))
+COLUMN_HALVES = ((0, U // 2), (U // 2, U))
+SHARES = ((0, 256, "scalar"), (512, 1024, "vector"), (256, 512, "scalar"))
 
 
 def tile_picked_gmem_tanh_lo_kernel(tc, xT, mem, w1, w2, offs, slot, out_0, out_1, out_2):
@@ -79,8 +80,8 @@ def tile_picked_gmem_tanh_lo_kernel(tc, xT, mem, w1, w2, offs, slot, out_0, out_
         interleave_x(nc.vector.tensor_copy, 0, 0, S)
         gather_x("vector", LAST, *first)
         gather_x("scalar", LAST, *second)
-        interleave_x(nc.vector.tensor_copy, 1, *first)
-        interleave_x(nc.scalar.copy, 1, *second)
+        interleave_x(nc.vector.tensor_copy, 1, *second)
+        interleave_x(nc.scalar.copy, 1, *first)
 
         w_bf = {(w, pair): keep.tile([P, 2, P, PACK], BF16, name=f"{w}_bf{pair}", align_bytes=64) for w in ("w1", "w2") for pair in range(2)}
 
@@ -134,36 +135,36 @@ def tile_picked_gmem_tanh_lo_kernel(tc, xT, mem, w1, w2, offs, slot, out_0, out_
         quantize_w("w2", 1, 2)
         quantize_w("w2", 2, PACK)
 
-        cand = keep.tile([P, PACK, S], F32, name="cand")
+        rows = [keep.tile([P, PACK, hi - lo], F32, name=f"rows{lo}") for lo, hi in COLUMN_HALVES]
+        cand = [keep.tile([P, S], F32, name=f"cand{t}")[:] for t in range(LAST)] + [rows[0][:, 2, :]]
         stay = [keep.tile([P, S], F32, name=f"stay{t}", tag=f"stay{t}", align_bytes=64) for t in range(PACK)]
         diff = [keep.tile([P, S], F32, name=f"diff{t}", tag=f"diff{t}", align_bytes=64) for t in range(PACK)]
-        kept = [keep.tile([P, S], F32, name=f"kept{t}", tag=f"kept{t}", align_bytes=64) for t in range(PACK)]
+        kept = [keep.tile([P, S], F32, name=f"kept{t}")[:] for t in range(LAST)] + [rows[1][:, 2, :]]
         new = keep.tile([P, LAST, S], F32, name="new")
 
         for lo, hi in LIST_HALVES:
-            nc.scalar.activation(cand[:, 0, lo:hi], product("w1", 0, f"bank{lo}", lo, hi)[:], ACT.Tanh)
+            nc.scalar.activation(cand[0][:, lo:hi], product("w1", 0, f"bank{lo}", lo, hi)[:], ACT.Tanh)
         for t in range(1, PACK):
-            nc.scalar.activation(cand[:, t, :], product("w1", t, f"bank{t}")[:], ACT.Tanh)
+            nc.scalar.activation(cand[t], product("w1", t, f"bank{t}")[:], ACT.Tanh)
         for t in range(PACK):
             nc.scalar.activation(stay[t][:], product("w2", t, f"bank{PACK + t}" if t else "bank0")[:], ACT.Sigmoid, scale=-1.0)
 
-        rows = [keep.tile([P, PACK, hi - lo], F32, name=f"rows{lo}") for lo, hi, engine in SHARES]
 
         for t in range(PACK):
             for lo, hi in LIST_HALVES:
-                nc.vector.tensor_tensor(diff[t][:, lo:hi], page[t][:].indirect(entries(slot_t, lo, hi)), cand[:, t, lo:hi], ALU.subtract)
+                nc.vector.tensor_tensor(diff[t][:, lo:hi], page[t][:].indirect(entries(slot_t, lo, hi)), cand[t][:, lo:hi], ALU.subtract)
             for lo, hi in LIST_HALVES:
                 nc.vector.tensor_tensor(kept[t][:, lo:hi], diff[t][:, lo:hi], stay[t][:, lo:hi], ALU.mult)
             if t < LAST:
                 for lo, hi in LIST_HALVES:
-                    nc.vector.tensor_tensor(new[:, t, lo:hi], kept[t][:, lo:hi], cand[:, t, lo:hi], ALU.add)
+                    nc.vector.tensor_tensor(new[:, t, lo:hi], kept[t][:, lo:hi], cand[t][:, lo:hi], ALU.add)
                 for lo, hi in LIST_HALVES:
                     nc.scalar.activation(page[t][:].indirect(entries(slot_t, lo, hi)), new[:, t, lo:hi], ACT.Copy)
             else:
-                nc.vector.tensor_tensor(page[t][:].indirect(slot_t[:]), kept[t][:], cand[:, t, :], ALU.add)
+                nc.vector.tensor_tensor(page[t][:].indirect(slot_t[:]), kept[t], cand[t], ALU.add)
             if t < 2:
-                for c, (lo, hi, engine) in enumerate(SHARES):
-                    nc.sync.dma_start(rows[c][:, t, :], page[t][:, lo:hi])
+                for h, (lo, hi) in enumerate(COLUMN_HALVES):
+                    nc.sync.dma_start(rows[h][:, t, :], page[t][:, lo:hi])
             nc.sync.dma_start(out_rows[:, t, :], page[t][:])
 
         y_codes = keep.tile([P, U], U32, name="y_codes", align_bytes=64)
@@ -171,12 +172,13 @@ def tile_picked_gmem_tanh_lo_kernel(tc, xT, mem, w1, w2, offs, slot, out_0, out_
         words = out_1.rearrange("z l c r -> (z l) (c r)").bitcast(I32)
         y_bf = [keep.tile([P, hi - lo, PACK], BF16, name=f"y_bf{lo}", align_bytes=64) for lo, hi, engine in SHARES]
         copies = {"scalar": nc.scalar.copy, "vector": nc.vector.tensor_copy}
-        for c in (1, 0, 2):
-            lo, hi, engine = SHARES[c]
-            nc.scalar.copy(rows[c][:, 2, :], page[2][:, lo:hi])
-            nc.vector.tensor_copy(rows[c][:, LAST, :], page[LAST][:, lo:hi])
+        for h, (lo, hi) in enumerate(COLUMN_HALVES):
+            for t in (LAST, 2):
+                nc.vector.tensor_copy(rows[h][:, t, :], page[t][:, lo:hi])
         for c, (lo, hi, engine) in enumerate(SHARES):
-            copies[engine](y_bf[c][:].rearrange("p (g i) t -> p g t i", i=4), rows[c][:].rearrange("p t (g i) -> p g t i", i=4))
+            h, first = divmod(lo, U // 2)
+            src = rows[h][:, :, first : first + hi - lo]
+            copies[engine](y_bf[c][:].rearrange("p (g i) t -> p g t i", i=4), src.rearrange("p t (g i) -> p g t i", i=4))
         for c, (lo, hi, engine) in enumerate(SHARES):
             nc.vector.quantize_mx(y_codes[:, lo:hi].bitcast(FP8X4), y_scales[:, lo:hi], y_bf[c][:].rearrange("p c t -> p (c t)"))
             nc.sync.dma_start(words[:, lo:hi], y_codes[:, lo:hi].bitcast(I32))

@@ -20,6 +20,7 @@ PACK = 4
 LAST = PACK - 1
 W_HALVES = ((0, N // 2), (N // 2, N))
 LIST_HALVES = ((0, S // 2), (S // 2, S))
+SCALAR_ENTRIES = (512, 512, 384, 0)
 COLUMN_HALVES = ((0, U // 2), (U // 2, U))
 SHARES = ((0, 256, "scalar"), (512, 1024, "vector"), (256, 512, "scalar"))
 
@@ -136,7 +137,7 @@ def tile_picked_gmem_tanh_lo_kernel(tc, xT, mem, w1, w2, offs, slot, out_0, out_
         quantize_w("w2", 2, PACK)
 
         rows = [keep.tile([P, PACK, hi - lo], F32, name=f"rows{lo}") for lo, hi in COLUMN_HALVES]
-        cand = [keep.tile([P, S], F32, name=f"cand{t}")[:] for t in range(LAST)] + [rows[0][:, 2, :]]
+        cand = [keep.tile([P, S], F32, name=f"cand{t}")[:] for t in range(PACK)]
         stay = [keep.tile([P, S], F32, name=f"stay{t}", tag=f"stay{t}", align_bytes=64) for t in range(PACK)]
         diff = [keep.tile([P, S], F32, name=f"diff{t}", tag=f"diff{t}", align_bytes=64) for t in range(PACK)]
         kept = [keep.tile([P, S], F32, name=f"kept{t}")[:] for t in range(LAST)] + [rows[1][:, 2, :]]
@@ -155,13 +156,14 @@ def tile_picked_gmem_tanh_lo_kernel(tc, xT, mem, w1, w2, offs, slot, out_0, out_
                 nc.vector.tensor_tensor(diff[t][:, lo:hi], page[t][:].indirect(entries(slot_t, lo, hi)), cand[t][:, lo:hi], ALU.subtract)
             for lo, hi in LIST_HALVES:
                 nc.vector.tensor_tensor(kept[t][:, lo:hi], diff[t][:, lo:hi], stay[t][:, lo:hi], ALU.mult)
-            if t < LAST:
-                for lo, hi in LIST_HALVES:
-                    nc.vector.tensor_tensor(new[:, t, lo:hi], kept[t][:, lo:hi], cand[t][:, lo:hi], ALU.add)
-                for lo, hi in LIST_HALVES:
-                    nc.scalar.activation(page[t][:].indirect(entries(slot_t, lo, hi)), new[:, t, lo:hi], ACT.Copy)
-            else:
-                nc.vector.tensor_tensor(page[t][:].indirect(slot_t[:]), kept[t], cand[t], ALU.add)
+            split = SCALAR_ENTRIES[t]
+            by_scalar = [(lo, min(hi, split)) for lo, hi in LIST_HALVES if lo < split]
+            for lo, hi in by_scalar:
+                nc.vector.tensor_tensor(new[:, t, lo:hi], kept[t][:, lo:hi], cand[t][:, lo:hi], ALU.add)
+            if split < S:
+                nc.vector.tensor_tensor(page[t][:].indirect(entries(slot_t, split, S)), kept[t][:, split:], cand[t][:, split:], ALU.add)
+            for lo, hi in by_scalar:
+                nc.scalar.activation(page[t][:].indirect(entries(slot_t, lo, hi)), new[:, t, lo:hi], ACT.Copy)
             if t < 2:
                 for h, (lo, hi) in enumerate(COLUMN_HALVES):
                     nc.sync.dma_start(rows[h][:, t, :], page[t][:, lo:hi])
@@ -172,9 +174,10 @@ def tile_picked_gmem_tanh_lo_kernel(tc, xT, mem, w1, w2, offs, slot, out_0, out_
         words = out_1.rearrange("z l c r -> (z l) (c r)").bitcast(I32)
         y_bf = [keep.tile([P, hi - lo, PACK], BF16, name=f"y_bf{lo}", align_bytes=64) for lo, hi, engine in SHARES]
         copies = {"scalar": nc.scalar.copy, "vector": nc.vector.tensor_copy}
+        copies["scalar"](rows[0][:, 2, :], page[2][:, : U // 2])
         for h, (lo, hi) in enumerate(COLUMN_HALVES):
-            for t in (LAST, 2):
-                nc.vector.tensor_copy(rows[h][:, t, :], page[t][:, lo:hi])
+            nc.vector.tensor_copy(rows[h][:, LAST, :], page[LAST][:, lo:hi])
+        nc.vector.tensor_copy(rows[1][:, 2, :], page[2][:, U // 2 :])
         for c, (lo, hi, engine) in enumerate(SHARES):
             h, first = divmod(lo, U // 2)
             src = rows[h][:, :, first : first + hi - lo]

@@ -20,7 +20,7 @@ PACK = 4
 LAST = PACK - 1
 W_HALVES = ((0, N // 2), (N // 2, N))
 LIST_HALVES = ((0, S // 2), (S // 2, S))
-SCALAR_ENTRIES = (512, 512, 384, 0)
+SPLIT = 384
 COLUMN_HALVES = ((0, U // 2), (U // 2, U))
 SHARES = ((0, 256, "scalar"), (512, 1024, "vector"), (256, 512, "scalar"))
 
@@ -140,7 +140,7 @@ def tile_picked_gmem_tanh_lo_kernel(tc, xT, mem, w1, w2, offs, slot, out_0, out_
         cand = [keep.tile([P, S], F32, name=f"cand{t}")[:] for t in range(PACK)]
         stay = [keep.tile([P, S], F32, name=f"stay{t}", tag=f"stay{t}", align_bytes=64) for t in range(PACK)]
         diff = [keep.tile([P, S], F32, name=f"diff{t}", tag=f"diff{t}", align_bytes=64) for t in range(PACK)]
-        kept = [keep.tile([P, S], F32, name=f"kept{t}")[:] for t in range(LAST)] + [rows[1][:, 2, :]]
+        kept = [keep.tile([P, S], F32, name=f"kept{t}")[:] for t in range(PACK)]
         new = keep.tile([P, LAST, S], F32, name="new")
 
         for lo, hi in LIST_HALVES:
@@ -151,22 +151,39 @@ def tile_picked_gmem_tanh_lo_kernel(tc, xT, mem, w1, w2, offs, slot, out_0, out_
             nc.scalar.activation(stay[t][:], product("w2", t, f"bank{PACK + t}" if t else "bank0")[:], ACT.Sigmoid, scale=-1.0)
 
 
-        for t in range(PACK):
+        def look_up_and_weigh(t):
             for lo, hi in LIST_HALVES:
                 nc.vector.tensor_tensor(diff[t][:, lo:hi], page[t][:].indirect(entries(slot_t, lo, hi)), cand[t][:, lo:hi], ALU.subtract)
             for lo, hi in LIST_HALVES:
                 nc.vector.tensor_tensor(kept[t][:, lo:hi], diff[t][:, lo:hi], stay[t][:, lo:hi], ALU.mult)
-            split = SCALAR_ENTRIES[t]
-            by_scalar = [(lo, min(hi, split)) for lo, hi in LIST_HALVES if lo < split]
-            for lo, hi in by_scalar:
-                nc.vector.tensor_tensor(new[:, t, lo:hi], kept[t][:, lo:hi], cand[t][:, lo:hi], ALU.add)
-            if split < S:
-                nc.vector.tensor_tensor(page[t][:].indirect(entries(slot_t, split, S)), kept[t][:, split:], cand[t][:, split:], ALU.add)
-            for lo, hi in by_scalar:
-                nc.scalar.activation(page[t][:].indirect(entries(slot_t, lo, hi)), new[:, t, lo:hi], ACT.Copy)
-            if t < 2:
-                for h, (lo, hi) in enumerate(COLUMN_HALVES):
-                    nc.sync.dma_start(rows[h][:, t, :], page[t][:, lo:hi])
+
+        def add(t, lo, hi):
+            nc.vector.tensor_tensor(new[:, t, lo:hi], kept[t][:, lo:hi], cand[t][:, lo:hi], ALU.add)
+
+        def scatter_on_scalar(t, lo, hi):
+            nc.scalar.activation(page[t][:].indirect(entries(slot_t, lo, hi)), new[:, t, lo:hi], ACT.Copy)
+
+        def add_and_scatter_on_vector(t, lo, hi):
+            nc.vector.tensor_tensor(page[t][:].indirect(entries(slot_t, lo, hi)), kept[t][:, lo:hi], cand[t][:, lo:hi], ALU.add)
+
+        for t in range(2):
+            look_up_and_weigh(t)
+            for lo, hi in LIST_HALVES:
+                add(t, lo, hi)
+            for lo, hi in LIST_HALVES:
+                scatter_on_scalar(t, lo, hi)
+            for h, (lo, hi) in enumerate(COLUMN_HALVES):
+                nc.sync.dma_start(rows[h][:, t, :], page[t][:, lo:hi])
+            nc.sync.dma_start(out_rows[:, t, :], page[t][:])
+        look_up_and_weigh(2)
+        add(2, 0, S // 2)
+        add_and_scatter_on_vector(2, SPLIT, S)
+        scatter_on_scalar(2, 0, S // 2)
+        look_up_and_weigh(LAST)
+        add(2, S // 2, SPLIT)
+        scatter_on_scalar(2, S // 2, SPLIT)
+        add_and_scatter_on_vector(LAST, 0, S)
+        for t in (2, LAST):
             nc.sync.dma_start(out_rows[:, t, :], page[t][:])
 
         y_codes = keep.tile([P, U], U32, name="y_codes", align_bytes=64)
@@ -174,10 +191,10 @@ def tile_picked_gmem_tanh_lo_kernel(tc, xT, mem, w1, w2, offs, slot, out_0, out_
         words = out_1.rearrange("z l c r -> (z l) (c r)").bitcast(I32)
         y_bf = [keep.tile([P, hi - lo, PACK], BF16, name=f"y_bf{lo}", align_bytes=64) for lo, hi, engine in SHARES]
         copies = {"scalar": nc.scalar.copy, "vector": nc.vector.tensor_copy}
-        copies["scalar"](rows[0][:, 2, :], page[2][:, : U // 2])
+        nc.scalar.copy(rows[0][:, 2, :], page[2][:, : U // 2])
+        nc.vector.tensor_copy(rows[1][:, 2, :], page[2][:, U // 2 :])
         for h, (lo, hi) in enumerate(COLUMN_HALVES):
             nc.vector.tensor_copy(rows[h][:, LAST, :], page[LAST][:, lo:hi])
-        nc.vector.tensor_copy(rows[1][:, 2, :], page[2][:, U // 2 :])
         for c, (lo, hi, engine) in enumerate(SHARES):
             h, first = divmod(lo, U // 2)
             src = rows[h][:, :, first : first + hi - lo]

@@ -20,9 +20,8 @@ PACK = 4
 LAST = PACK - 1
 W_HALVES = ((0, N // 2), (N // 2, N))
 LIST_HALVES = ((0, S // 2), (S // 2, S))
-SPLIT = 384
-COLUMN_HALVES = ((0, U // 2), (U // 2, U))
-SHARES = ((0, 256, "scalar"), (512, 1024, "vector"), (256, 512, "scalar"))
+SPLIT = 416
+RANGES = ((0, 256), (256, 512), (512, 1024))
 
 
 def tile_picked_gmem_tanh_lo_kernel(tc, xT, mem, w1, w2, offs, slot, out_0, out_1, out_2):
@@ -136,7 +135,7 @@ def tile_picked_gmem_tanh_lo_kernel(tc, xT, mem, w1, w2, offs, slot, out_0, out_
         quantize_w("w2", 1, 2)
         quantize_w("w2", 2, PACK)
 
-        rows = [keep.tile([P, PACK, hi - lo], F32, name=f"rows{lo}") for lo, hi in COLUMN_HALVES]
+        rows = [keep.tile([P, PACK, hi - lo], F32, name=f"rows{lo}") for lo, hi in RANGES]
         cand = [keep.tile([P, S], F32, name=f"cand{t}")[:] for t in range(PACK)]
         stay = [keep.tile([P, S], F32, name=f"stay{t}", tag=f"stay{t}", align_bytes=64) for t in range(PACK)]
         diff = [keep.tile([P, S], F32, name=f"diff{t}", tag=f"diff{t}", align_bytes=64) for t in range(PACK)]
@@ -172,7 +171,7 @@ def tile_picked_gmem_tanh_lo_kernel(tc, xT, mem, w1, w2, offs, slot, out_0, out_
                 add(t, lo, hi)
             for lo, hi in LIST_HALVES:
                 scatter_on_scalar(t, lo, hi)
-            for h, (lo, hi) in enumerate(COLUMN_HALVES):
+            for h, (lo, hi) in enumerate(RANGES):
                 nc.sync.dma_start(rows[h][:, t, :], page[t][:, lo:hi])
             nc.sync.dma_start(out_rows[:, t, :], page[t][:])
         look_up_and_weigh(2)
@@ -189,19 +188,25 @@ def tile_picked_gmem_tanh_lo_kernel(tc, xT, mem, w1, w2, offs, slot, out_0, out_
         y_codes = keep.tile([P, U], U32, name="y_codes", align_bytes=64)
         y_scales = keep.tile([P, U], U8, name="y_scales", align_bytes=64)
         words = out_1.rearrange("z l c r -> (z l) (c r)").bitcast(I32)
-        y_bf = [keep.tile([P, hi - lo, PACK], BF16, name=f"y_bf{lo}", align_bytes=64) for lo, hi, engine in SHARES]
-        copies = {"scalar": nc.scalar.copy, "vector": nc.vector.tensor_copy}
-        nc.scalar.copy(rows[0][:, 2, :], page[2][:, : U // 2])
-        nc.vector.tensor_copy(rows[1][:, 2, :], page[2][:, U // 2 :])
-        for h, (lo, hi) in enumerate(COLUMN_HALVES):
-            nc.vector.tensor_copy(rows[h][:, LAST, :], page[LAST][:, lo:hi])
-        for c, (lo, hi, engine) in enumerate(SHARES):
-            h, first = divmod(lo, U // 2)
-            src = rows[h][:, :, first : first + hi - lo]
-            copies[engine](y_bf[c][:].rearrange("p (g i) t -> p g t i", i=4), src.rearrange("p t (g i) -> p g t i", i=4))
-        for c, (lo, hi, engine) in enumerate(SHARES):
-            nc.vector.quantize_mx(y_codes[:, lo:hi].bitcast(FP8X4), y_scales[:, lo:hi], y_bf[c][:].rearrange("p c t -> p (c t)"))
-            nc.sync.dma_start(words[:, lo:hi], y_codes[:, lo:hi].bitcast(I32))
+        y_bf = [keep.tile([P, hi - lo, PACK], BF16, name=f"y_bf{lo}", align_bytes=64) for lo, hi in RANGES]
+
+        def carry(copy, t, c):
+            copy(rows[c][:, t, :], page[t][:, slice(*RANGES[c])])
+
+        def weave(copy, c):
+            copy(y_bf[c][:].rearrange("p (g i) t -> p g t i", i=4), rows[c][:].rearrange("p t (g i) -> p g t i", i=4))
+
+        for c in (0, 1):
+            carry(nc.scalar.copy, 2, c)
+        carry(nc.vector.tensor_copy, 2, 2)
+        for c in (0, 2, 1):
+            carry(nc.vector.tensor_copy, LAST, c)
+        for c in range(3):
+            weave(nc.scalar.copy if c < 2 else nc.vector.tensor_copy, c)
+        for c in (0, 2, 1):
+            cols = slice(*RANGES[c])
+            nc.vector.quantize_mx(y_codes[:, cols].bitcast(FP8X4), y_scales[:, cols], y_bf[c][:].rearrange("p c t -> p (c t)"))
+            nc.sync.dma_start(words[:, cols], y_codes[:, cols].bitcast(I32))
         scale_rows = out_2.rearrange("z q c -> (z q) c").bitcast(I32)
         for q in range(P // 32):
             queue = nc.scalar if q % 2 else nc.sync

@@ -20,7 +20,7 @@ PACK = 4
 LAST = PACK - 1
 W_HALVES = ((0, N // 2), (N // 2, N))
 LIST_HALVES = ((0, S // 2), (S // 2, S))
-SPLIT = 416
+SPLIT = 384
 RANGES = ((0, 256), (256, 512), (512, 1024))
 
 

@@ -20,7 +20,8 @@ PACK = 4
 LAST = PACK - 1
 W_HALVES = ((0, N // 2), (N // 2, N))
 LIST_HALVES = ((0, S // 2), (S // 2, S))
-SPLIT = 384
+SPLIT = 448
+FIRST = 384
 RANGES = ((0, 256), (256, 512), (512, 1024))
 
 
@@ -75,13 +76,15 @@ def tile_picked_gmem_tanh_lo_kernel(tc, xT, mem, w1, w2, offs, slot, out_0, out_
 
         first, second = LIST_HALVES
         gather_x("vector", 0, 0, S)
-        gather_x("scalar", 1, 0, S)
+        gather_x("vector", 1, *first)
+        gather_x("scalar", 1, *second)
         gather_x("scalar", 2, 0, S)
         interleave_x(nc.vector.tensor_copy, 0, 0, S)
         gather_x("vector", LAST, *first)
         gather_x("scalar", LAST, *second)
         interleave_x(nc.vector.tensor_copy, 1, *second)
-        interleave_x(nc.scalar.copy, 1, *first)
+        interleave_x(nc.scalar.copy, 1, 0, S // 4)
+        interleave_x(nc.vector.tensor_copy, 1, S // 4, S // 2)
 
         w_bf = {(w, pair): keep.tile([P, 2, P, PACK], BF16, name=f"{w}_bf{pair}", align_bytes=64) for w in ("w1", "w2") for pair in range(2)}
 
@@ -120,7 +123,7 @@ def tile_picked_gmem_tanh_lo_kernel(tc, xT, mem, w1, w2, offs, slot, out_0, out_
             return acc
 
         regroup_w(nc.scalar.copy, "w1", 0, 0)
-        for lo, hi in LIST_HALVES:
+        for lo, hi in (second, first):
             nc.vector.quantize_mx(x_codes[:, lo:hi].bitcast(FP8X4), x_scales[:, lo:hi], x_bf[:, lo:hi, :].rearrange("p c j -> p (c j)"))
         regroup_w(nc.vector.tensor_copy, "w1", 1, 0)
         for h in range(2):
@@ -136,18 +139,18 @@ def tile_picked_gmem_tanh_lo_kernel(tc, xT, mem, w1, w2, offs, slot, out_0, out_
         quantize_w("w2", 2, PACK)
 
         rows = [keep.tile([P, PACK, hi - lo], F32, name=f"rows{lo}") for lo, hi in RANGES]
-        cand = [keep.tile([P, S], F32, name=f"cand{t}")[:] for t in range(PACK)]
+        cand_all = keep.tile([P, PACK * S], F32, name="cand_all")
+        kept_all = keep.tile([P, PACK * S], F32, name="kept_all")
+        new_all = keep.tile([P, LAST * S], F32, name="new_all")
+        cand, kept = ([whole[:, t * S : (t + 1) * S] for t in range(PACK)] for whole in (cand_all, kept_all))
         stay = [keep.tile([P, S], F32, name=f"stay{t}", tag=f"stay{t}", align_bytes=64) for t in range(PACK)]
         diff = [keep.tile([P, S], F32, name=f"diff{t}", tag=f"diff{t}", align_bytes=64) for t in range(PACK)]
-        kept = [keep.tile([P, S], F32, name=f"kept{t}")[:] for t in range(PACK)]
-        new = keep.tile([P, LAST, S], F32, name="new")
 
-        for lo, hi in LIST_HALVES:
-            nc.scalar.activation(cand[0][:, lo:hi], product("w1", 0, f"bank{lo}", lo, hi)[:], ACT.Tanh)
-        for t in range(1, PACK):
-            nc.scalar.activation(cand[t], product("w1", t, f"bank{t}")[:], ACT.Tanh)
         for t in range(PACK):
-            nc.scalar.activation(stay[t][:], product("w2", t, f"bank{PACK + t}" if t else "bank0")[:], ACT.Sigmoid, scale=-1.0)
+            for lo, hi in LIST_HALVES if t < 2 else ((0, S),):
+                nc.scalar.activation(cand[t][:, lo:hi], product("w1", t, f"bank{t}_{lo}", lo, hi)[:], ACT.Tanh)
+        for t, bank in enumerate(("bank0_0", f"bank0_{S // 2}", "bank6", "bank7")):
+            nc.scalar.activation(stay[t][:], product("w2", t, bank)[:], ACT.Sigmoid, scale=-1.0)
 
 
         def look_up_and_weigh(t):
@@ -157,22 +160,27 @@ def tile_picked_gmem_tanh_lo_kernel(tc, xT, mem, w1, w2, offs, slot, out_0, out_
                 nc.vector.tensor_tensor(kept[t][:, lo:hi], diff[t][:, lo:hi], stay[t][:, lo:hi], ALU.mult)
 
         def add(t, lo, hi):
-            nc.vector.tensor_tensor(new[:, t, lo:hi], kept[t][:, lo:hi], cand[t][:, lo:hi], ALU.add)
+            cols = slice(t * S + lo, t * S + hi)
+            nc.vector.tensor_tensor(new_all[:, cols], kept_all[:, cols], cand_all[:, cols], ALU.add)
 
         def scatter_on_scalar(t, lo, hi):
-            nc.scalar.activation(page[t][:].indirect(entries(slot_t, lo, hi)), new[:, t, lo:hi], ACT.Copy)
+            nc.scalar.activation(page[t][:].indirect(entries(slot_t, lo, hi)), new_all[:, t * S + lo : t * S + hi], ACT.Copy)
 
         def add_and_scatter_on_vector(t, lo, hi):
             nc.vector.tensor_tensor(page[t][:].indirect(entries(slot_t, lo, hi)), kept[t][:, lo:hi], cand[t][:, lo:hi], ALU.add)
 
-        for t in range(2):
-            look_up_and_weigh(t)
-            for lo, hi in LIST_HALVES:
-                add(t, lo, hi)
-            for lo, hi in LIST_HALVES:
-                scatter_on_scalar(t, lo, hi)
-            for h, (lo, hi) in enumerate(RANGES):
-                nc.sync.dma_start(rows[h][:, t, :], page[t][:, lo:hi])
+        look_up_and_weigh(0)
+        add(0, 0, S // 2)
+        add(0, S // 2, FIRST)
+        scatter_on_scalar(0, 0, FIRST)
+        look_up_and_weigh(1)
+        add(0, FIRST, S + S // 2)
+        add(1, S // 2, S)
+        scatter_on_scalar(1, 0, S // 2)
+        for t, done in ((0, FIRST), (1, S // 2)):
+            scatter_on_scalar(t, done, S)
+            for c, (lo, hi) in enumerate(RANGES):
+                nc.sync.dma_start(rows[c][:, t, :], page[t][:, lo:hi])
             nc.sync.dma_start(out_rows[:, t, :], page[t][:])
         look_up_and_weigh(2)
         add(2, 0, S // 2)
@@ -197,10 +205,9 @@ def tile_picked_gmem_tanh_lo_kernel(tc, xT, mem, w1, w2, offs, slot, out_0, out_
             copy(y_bf[c][:].rearrange("p (g i) t -> p g t i", i=4), rows[c][:].rearrange("p t (g i) -> p g t i", i=4))
 
         for c in (0, 1):
-            carry(nc.scalar.copy, 2, c)
-        carry(nc.vector.tensor_copy, 2, 2)
-        for c in (0, 2, 1):
-            carry(nc.vector.tensor_copy, LAST, c)
+            carry(nc.scalar.copy, LAST, c)
+        for t, c in ((2, 0), (2, 2), (LAST, 2), (2, 1)):
+            carry(nc.vector.tensor_copy, t, c)
         for c in range(3):
             weave(nc.scalar.copy if c < 2 else nc.vector.tensor_copy, c)
         for c in (0, 2, 1):

@@ -20,7 +20,7 @@ PACK = 4
 LAST = PACK - 1
 W_HALVES = ((0, N // 2), (N // 2, N))
 LIST_HALVES = ((0, S // 2), (S // 2, S))
-SPLIT = 448
+SPLIT = 416
 FIRST = 384
 RANGES = ((0, 256), (256, 512), (512, 1024))
 
@@ -134,8 +134,7 @@ def tile_picked_gmem_tanh_lo_kernel(tc, xT, mem, w1, w2, offs, slot, out_0, out_
         for h in range(2):
             for pair in range(2):
                 regroup_w(nc.vector.tensor_copy, "w2", h, pair)
-        quantize_w("w2", 0, 1)
-        quantize_w("w2", 1, 2)
+        quantize_w("w2", 0, 2)
         quantize_w("w2", 2, PACK)
 
         rows = [keep.tile([P, PACK, hi - lo], F32, name=f"rows{lo}") for lo, hi in RANGES]
@@ -150,7 +149,9 @@ def tile_picked_gmem_tanh_lo_kernel(tc, xT, mem, w1, w2, offs, slot, out_0, out_
             for lo, hi in LIST_HALVES if t < 2 else ((0, S),):
                 nc.scalar.activation(cand[t][:, lo:hi], product("w1", t, f"bank{t}_{lo}", lo, hi)[:], ACT.Tanh)
         for t, bank in enumerate(("bank0_0", f"bank0_{S // 2}", "bank6", "bank7")):
-            nc.scalar.activation(stay[t][:], product("w2", t, bank)[:], ACT.Sigmoid, scale=-1.0)
+            acc = product("w2", t, bank)
+            for lo, hi in LIST_HALVES if t == 0 else ((0, S),):
+                nc.scalar.activation(stay[t][:, lo:hi], acc[:, lo:hi], ACT.Sigmoid, scale=-1.0)
 
 
         def look_up_and_weigh(t):

@@ -203,7 +203,7 @@ def tile_picked_gmem_tanh_lo_kernel(tc, xT, mem, w1, w2, offs, slot, out_0, out_
             copy(rows[c][:, t, :], page[t][:, slice(*RANGES[c])])
 
         def weave(copy, c):
-            copy(y_bf[c][:].rearrange("p (g i) t -> p g t i", i=4), rows[c][:].rearrange("p t (g i) -> p g t i", i=4))
+            copy(y_bf[c][:].rearrange("p (g i) t -> p g t i", i=2), rows[c][:].rearrange("p t (g i) -> p g t i", i=2))
 
         for c in (0, 1):
             carry(nc.scalar.copy, LAST, c)

@@ -214,7 +214,8 @@ def tile_picked_gmem_tanh_lo_kernel(tc, xT, mem, w1, w2, offs, slot, out_0, out_
         for c in (0, 2, 1):
             cols = slice(*RANGES[c])
             nc.vector.quantize_mx(y_codes[:, cols].bitcast(FP8X4), y_scales[:, cols], y_bf[c][:].rearrange("p c t -> p (c t)"))
-            nc.sync.dma_start(words[:, cols], y_codes[:, cols].bitcast(I32))
+            queue = nc.scalar if c == 1 else nc.sync
+            queue.dma_start(words[:, cols], y_codes[:, cols].bitcast(I32))
         scale_rows = out_2.rearrange("z q c -> (z q) c").bitcast(I32)
         for q in range(P // 32):
             queue = nc.scalar if q % 2 else nc.sync

from contextlib import ExitStack

import concourse.mybir as mybir

K, T, S, N, U = 512, 1024, 512, 512, 1024
FLOPS = 2 * 2 * K * N * S

F32 = mybir.dt.float32
BF16 = mybir.dt.bfloat16
I32 = mybir.dt.int32
U32 = mybir.dt.uint32
U16 = mybir.dt.uint16
U8 = mybir.dt.uint8
FP8X4 = mybir.dt.float8_e4m3fn_x4
ALU = mybir.AluOpType
ACT = mybir.ActivationFunctionType

P = 128
PACK = 4
LAST = PACK - 1
W_HALVES = ((0, N // 2), (N // 2, N))
LIST_HALVES = ((0, S // 2), (S // 2, S))
SPLIT = 416
FIRST = 384
RANGES = ((0, 256), (256, 512), (512, 1024))


def tile_picked_gmem_tanh_lo_kernel(tc, xT, mem, w1, w2, offs, slot, out_0, out_1, out_2):
    nc = tc.nc
    with ExitStack() as ctx:
        keep = ctx.enter_context(tc.tile_pool(name="keep", bufs=1))
        psum = ctx.enter_context(tc.psum_pool(name="psum", bufs=1))

        offs_t = keep.tile([P, S // 16], U16, name="offs_t")
        slot_t = keep.tile([P, S // 16], U16, name="slot_t")
        x_raw = [keep.tile([P, T], F32, name=f"x_raw{j}") for j in range(PACK)]
        w_raw = {(w, h): keep.tile([P, PACK, N // 2], F32, name=f"{w}_raw{h}") for w in ("w1", "w2") for h in range(2)}
        page = [keep.tile([P, U], F32, name=f"page{t}") for t in range(PACK)]

        x_rows = xT.rearrange("(p j) c -> p j c", j=PACK)
        mem_rows = mem.rearrange("(p t) c -> p t c", t=PACK)
        out_rows = out_0.rearrange("(p t) c -> p t c", t=PACK)

        for j in range(PACK):
            nc.sync.dma_start(x_raw[j][:], x_rows[:, j, :])
            if j == 0:
                nc.sync.dma_start(offs_t[:], offs)
        for which, w in (("w1", w1), ("w2", w2)):
            w_rows = w.rearrange("(p j) c -> p j c", j=PACK)
            for h, (lo, hi) in enumerate(W_HALVES):
                nc.sync.dma_start(w_raw[which, h][:], w_rows[:, :, lo:hi])
        nc.sync.dma_start(slot_t[:], slot)
        for t in range(PACK):
            nc.sync.dma_start(page[t][:], mem_rows[:, t, :])

        warm_in = keep.tile([P, 1], F32, name="warm_in")
        warm_out = keep.tile([P, 1], F32, name="warm_out")
        nc.vector.memset(warm_in[:], 0.0)
        nc.scalar.activation(warm_out[:], warm_in[:], ACT.Sigmoid)

        def entries(offsets, lo, hi):
            return offsets[:, lo // 16 : hi // 16]

        picked = [keep.tile([P, 2, S], F32, name=f"picked{pair}") for pair in range(2)]
        x_bf = keep.tile([P, S, PACK], BF16, name="x_bf", align_bytes=64)

        def interleave_x(copy, pair, lo, hi):
            copy(x_bf[:, lo:hi, 2 * pair : 2 * pair + 2], picked[pair][:, :, lo:hi].rearrange("p e c -> p c e"))

        def gather_x(engine, j, lo, hi):
            dst, src = picked[j // 2][:, j % 2, lo:hi], x_raw[j][:].indirect(entries(offs_t, lo, hi))
            if engine == "vector":
                nc.vector.tensor_copy(dst, src)
            else:
                nc.scalar.activation(dst, src, ACT.Copy)

        first, second = LIST_HALVES
        gather_x("vector", 0, 0, S)
        gather_x("vector", 1, *first)
        gather_x("scalar", 1, *second)
        gather_x("scalar", 2, 0, S)
        interleave_x(nc.vector.tensor_copy, 0, 0, S)
        gather_x("vector", LAST, *first)
        gather_x("scalar", LAST, *second)
        interleave_x(nc.vector.tensor_copy, 1, *second)
        interleave_x(nc.scalar.copy, 1, 0, S // 4)
        interleave_x(nc.vector.tensor_copy, 1, S // 4, S // 2)

        w_bf = {(w, pair): keep.tile([P, 2, P, PACK], BF16, name=f"{w}_bf{pair}", align_bytes=64) for w in ("w1", "w2") for pair in range(2)}

        def regroup_w(copy, which, h, pair):
            src = w_raw[which, h][:].rearrange("p j (m t) -> p m j t", t=PACK)
            dst = w_bf[which, pair][:].rearrange("p i m j -> p m j i")
            copy(dst[:, h * P // 2 : (h + 1) * P // 2], src[:, :, :, 2 * pair : 2 * pair + 2])

        stationary = {}

        def quantize_w(which, t0, t1):
            width = (t1 - t0) * P
            codes = keep.tile([P, width], U32, name=f"{which}_codes{t0}", align_bytes=64)
            scales = keep.tile([P, width], U8, name=f"{which}_scales{t0}", align_bytes=64)
            for t in range(t0, t1):
                cols = slice((t - t0) * P, (t - t0 + 1) * P)
                stationary[which, t] = (codes[:, cols], scales[:, cols])
            values = w_bf[which, t0 // 2][:, t0 % 2 : t0 % 2 + t1 - t0, :, :]
            nc.vector.quantize_mx(codes[:].bitcast(FP8X4), scales[:], values.rearrange("p t m j -> p (t m j)"))

        x_codes = keep.tile([P, S], U32, name="x_codes", align_bytes=64)
        x_scales = keep.tile([P, S], U8, name="x_scales", align_bytes=64)

        def product(which, t, bank, lo=0, hi=S):
            acc = psum.tile([P, hi - lo], F32, name=f"{which}_acc{t}_{lo}", tag=bank)
            codes, scales = stationary[which, t]
            nc.tensor.matmul_mx(
                acc[:],
                lhsT=codes.bitcast(FP8X4),
                lhsT_scale=scales,
                rhs=x_codes[:, lo:hi].bitcast(FP8X4),
                rhs_scale=x_scales[:, lo:hi],
                start=True,
                stop=True,
            )
            return acc

        regroup_w(nc.scalar.copy, "w1", 0, 0)
        for lo, hi in (second, first):
            nc.vector.quantize_mx(x_codes[:, lo:hi].bitcast(FP8X4), x_scales[:, lo:hi], x_bf[:, lo:hi, :].rearrange("p c j -> p (c j)"))
        regroup_w(nc.vector.tensor_copy, "w1", 1, 0)
        for h in range(2):
            regroup_w(nc.scalar.copy, "w1", h, 1)
        quantize_w("w1", 0, 1)
        quantize_w("w1", 1, 2)
        quantize_w("w1", 2, PACK)
        for h in range(2):
            for pair in range(2):
                regroup_w(nc.vector.tensor_copy, "w2", h, pair)
        quantize_w("w2", 0, 2)
        quantize_w("w2", 2, PACK)

        rows = [keep.tile([P, PACK, hi - lo], F32, name=f"rows{lo}") for lo, hi in RANGES]
        cand_all = keep.tile([P, PACK * S], F32, name="cand_all")
        kept_all = keep.tile([P, PACK * S], F32, name="kept_all")
        new_all = keep.tile([P, LAST * S], F32, name="new_all")
        cand, kept = ([whole[:, t * S : (t + 1) * S] for t in range(PACK)] for whole in (cand_all, kept_all))
        stay = [keep.tile([P, S], F32, name=f"stay{t}", tag=f"stay{t}", align_bytes=64) for t in range(PACK)]
        diff = [keep.tile([P, S], F32, name=f"diff{t}", tag=f"diff{t}", align_bytes=64) for t in range(PACK)]

        for t in range(PACK):
            for lo, hi in LIST_HALVES if t < 2 else ((0, S),):
                nc.scalar.activation(cand[t][:, lo:hi], product("w1", t, f"bank{t}_{lo}", lo, hi)[:], ACT.Tanh)
        for t, bank in enumerate(("bank0_0", f"bank0_{S // 2}", "bank6", "bank7")):
            acc = product("w2", t, bank)
            for lo, hi in LIST_HALVES if t == 0 else ((0, S),):
                nc.scalar.activation(stay[t][:, lo:hi], acc[:, lo:hi], ACT.Sigmoid, scale=-1.0)


        def look_up_and_weigh(t):
            for lo, hi in LIST_HALVES:
                nc.vector.tensor_tensor(diff[t][:, lo:hi], page[t][:].indirect(entries(slot_t, lo, hi)), cand[t][:, lo:hi], ALU.subtract)
            for lo, hi in LIST_HALVES:
                nc.vector.tensor_tensor(kept[t][:, lo:hi], diff[t][:, lo:hi], stay[t][:, lo:hi], ALU.mult)

        def add(t, lo, hi):
            cols = slice(t * S + lo, t * S + hi)
            nc.vector.tensor_tensor(new_all[:, cols], kept_all[:, cols], cand_all[:, cols], ALU.add)

        def scatter_on_scalar(t, lo, hi):
            nc.scalar.activation(page[t][:].indirect(entries(slot_t, lo, hi)), new_all[:, t * S + lo : t * S + hi], ACT.Copy)

        def add_and_scatter_on_vector(t, lo, hi):
            nc.vector.tensor_tensor(page[t][:].indirect(entries(slot_t, lo, hi)), kept[t][:, lo:hi], cand[t][:, lo:hi], ALU.add)

        look_up_and_weigh(0)
        add(0, 0, S // 2)
        add(0, S // 2, FIRST)
        scatter_on_scalar(0, 0, FIRST)
        look_up_and_weigh(1)
        add(0, FIRST, S + S // 2)
        add(1, S // 2, S)
        scatter_on_scalar(1, 0, S // 2)
        for t, done in ((0, FIRST), (1, S // 2)):
            scatter_on_scalar(t, done, S)
            for c, (lo, hi) in enumerate(RANGES):
                nc.sync.dma_start(rows[c][:, t, :], page[t][:, lo:hi])
            nc.sync.dma_start(out_rows[:, t, :], page[t][:])
        look_up_and_weigh(2)
        add(2, 0, S // 2)
        add_and_scatter_on_vector(2, SPLIT, S)
        scatter_on_scalar(2, 0, S // 2)
        look_up_and_weigh(LAST)
        add(2, S // 2, SPLIT)
        scatter_on_scalar(2, S // 2, SPLIT)
        add_and_scatter_on_vector(LAST, 0, S)
        for t in (2, LAST):
            nc.sync.dma_start(out_rows[:, t, :], page[t][:])

        y_codes = keep.tile([P, U], U32, name="y_codes", align_bytes=64)
        y_scales = keep.tile([P, U], U8, name="y_scales", align_bytes=64)
        words = out_1.rearrange("z l c r -> (z l) (c r)").bitcast(I32)
        y_bf = [keep.tile([P, hi - lo, PACK], BF16, name=f"y_bf{lo}", align_bytes=64) for lo, hi in RANGES]

        def carry(copy, t, c):
            copy(rows[c][:, t, :], page[t][:, slice(*RANGES[c])])

        def weave(copy, c):
            copy(y_bf[c][:].rearrange("p (g i) t -> p g t i", i=2), rows[c][:].rearrange("p t (g i) -> p g t i", i=2))

        for c in (0, 1):
            carry(nc.scalar.copy, LAST, c)
        for t, c in ((2, 0), (2, 2), (LAST, 2), (2, 1)):
            carry(nc.vector.tensor_copy, t, c)
        for c in range(3):
            weave(nc.scalar.copy if c < 2 else nc.vector.tensor_copy, c)
        for c in (0, 2, 1):
            cols = slice(*RANGES[c])
            nc.vector.quantize_mx(y_codes[:, cols].bitcast(FP8X4), y_scales[:, cols], y_bf[c][:].rearrange("p c t -> p (c t)"))
            queue = nc.scalar if c == 1 else nc.sync
            queue.dma_start(words[:, cols], y_codes[:, cols].bitcast(I32))
        scale_rows = out_2.rearrange("z q c -> (z q) c").bitcast(I32)
        for q in range(P // 32):
            queue = nc.scalar if q % 2 else nc.sync
            queue.dma_start(scale_rows[4 * q : 4 * q + 4, :], y_scales[32 * q : 32 * q + 4, :].bitcast(I32))
